import numpy as np
import ml_dtypes


def mxq(x, axis, fmt="e4m3"):
    dtype, down = {"e4m3": (ml_dtypes.float8_e4m3fn, 7), "e5m2": (ml_dtypes.float8_e5m2, 14)}[fmt]
    v = np.moveaxis(np.asarray(x, np.float32).astype(ml_dtypes.bfloat16).astype(np.float64), axis, -1)
    blocks = v.reshape(v.shape[:-1] + (-1, 32))
    amax = np.abs(blocks).max(-1, keepdims=True)
    byte = np.maximum(np.where(amax > 0, np.frexp(amax)[1] - 1 + 127, 0) - down, 1)
    scale = np.exp2(byte - 127.0)
    codes = (blocks / scale).astype(np.float32).astype(dtype).astype(np.float64)
    return np.moveaxis((codes * scale).reshape(v.shape), -1, axis)


WIDE = False


def mx_kscale(k):
    if not WIDE:
        return np.ones(k)
    levels = np.array([10, -10, 5, -5, 0])
    if k % 512:
        return np.exp2(np.random.permutation(np.resize(levels, k // 32))).repeat(32)
    a = np.empty((k // 512, 16))
    for p in range(k // 512):
        a[p, :8] = np.random.permutation(np.resize(levels, 8))
        for g in range(8):
            far = levels[np.abs(levels - a[p, g]) >= 10]
            a[p, g + 8] = far[np.random.randint(len(far))]
    return np.exp2(a.ravel()).repeat(32)


def f64(x):
    return np.asarray(x).astype(np.float64)


def striped(idx):
    return np.tile(idx.reshape(-1, 16).T, (8, 1)).astype(np.uint16)


def unstriped(offs):
    return offs[:16].T.reshape(-1).astype(np.int64)


def pack_weight(w):
    k, n = w.shape
    w = f64(np.asarray(w, np.float32).astype(ml_dtypes.bfloat16)).reshape(k // 32, 32, n)
    amax = np.abs(w).max(1)
    byte = np.clip(np.where(amax > 0, np.frexp(amax)[1] - 1 + 127 - 7, 1), 1, 254)
    scaled = (w * np.exp2(127.0 - byte)[:, None, :]).reshape(k, n).astype(np.float32)
    words = np.ascontiguousarray(scaled.reshape(k // 512, 128, 4, n).transpose(0, 1, 3, 2)).astype(ml_dtypes.float8_e4m3fn).view(np.uint8)
    return words, np.ascontiguousarray(byte.astype(np.uint8).reshape(k // 512, 16, n))


def unpack_weight(words, scales):
    g, p, n, _ = words.shape
    vals = np.ascontiguousarray(words).view(ml_dtypes.float8_e4m3fn).astype(np.float64) * np.repeat(np.exp2(scales.astype(np.float64) - 127.0), 8, axis=1)[..., None]
    return vals.transpose(0, 1, 3, 2).reshape(g * 512, n)


K, T, S, D, H, R = 1024, 4096, 1024, 4, 512, 512
P = 2 ** 7


def setup_inputs():
    n = np.random.standard_normal
    s = mx_kscale(K)[:, None]
    u = mx_kscale(H)
    packed_xT = pack_weight(n((K, T)) * s)
    return {
        "x_words": packed_xT[0],
        "x_scales": packed_xT[1],
        "w1": (n((K, H)) / np.sqrt(K) / s * u).astype(np.float32),
        "pos": (0.5 * n((H, S)) * u[:, None]).astype(np.float32),
        "mixw": (np.tile(np.random.uniform(0.1, 0.5, S), (P, 1))).astype(np.float32),
        "qT": (n((H, R)) / np.sqrt(H) / u[:, None]).astype(np.float32),
        "offs": striped(np.random.permutation(T)[:S]),
    }


def reference(x_words, x_scales, w1, pos, mixw, qT, offs):
    qTq = mxq(f64(qT), 0, "e4m3")
    xq = unpack_weight(x_words, x_scales)[:, unstriped(offs)]
    y = ((mxq(f64(w1), 0, "e4m3").T @ xq) + f64(pos)) * f64(mixw)[:1]
    kc = y.reshape(len(y), -1, D).sum(axis=2)
    sc = qTq.T @ mxq(kc, 0, "e4m3")
    ex = np.exp(sc - sc.max(axis=1, keepdims=True))
    return ex / ex.sum(axis=1, keepdims=True)

@@ -1,0 +1,222 @@
+from contextlib import ExitStack
+
+import concourse.mybir as mybir
+from concourse.masks import make_identity
+
+K, T, S, D, H, R = 1024, 4096, 1024, 4, 512, 512
+V = S // D
+FLOPS = 2 * K * H * S + 2 * H * R * V
+
+F32 = mybir.dt.float32
+BF16 = mybir.dt.bfloat16
+I32 = mybir.dt.int32
+U32 = mybir.dt.uint32
+U16 = mybir.dt.uint16
+U8 = mybir.dt.uint8
+FP8X4 = mybir.dt.float8_e4m3fn_x4
+ALU = mybir.AluOpType
+ACT = mybir.ActivationFunctionType
+AX = mybir.AxisListType
+
+P = 128
+PACK = 4
+K_PASS = P * PACK
+PASSES = K // K_PASS
+HALVES = V // P
+HALF = S // HALVES
+QTILES = R // P
+
+
+def tile_picked_ycblk_wts_p_kernel(
+    tc, x_words, x_scales, w1, pos, mixw, qT, offs, out
+):
+    nc = tc.nc
+    with ExitStack() as ctx:
+        keep = ctx.enter_context(tc.tile_pool(name="keep", bufs=1))
+        psum = ctx.enter_context(tc.psum_pool(name="psum", bufs=1))
+
+        def sb(name, shape, dtype, tag=None):
+            return keep.tile(shape, dtype, name=name, tag=tag or name, align_bytes=64)
+
+        def bank(index, shape):
+            return psum.tile(shape, F32, name="bank%d" % index, tag="bank%d" % index)
+
+        offsets = keep.tile([P, S // 16], U16, name="offsets")
+
+        warm_in = sb("warm_in", [P, 1], F32)
+        warm_out = sb("warm_out", [P, 1], F32)
+        nc.vector.memset(warm_in[:], 0.0)
+        nc.scalar.activation(out=warm_out[:], in_=warm_in[:], func=ACT.Exp)
+
+        ident = sb("ident", [P, P], F32)
+        make_identity(nc, ident[:])
+
+        scale_window = sb("scale_window", [P, T], U8)
+        nc.vector.memset(scale_window[:].bitcast(I32), 0)
+
+        pos_view = pos.rearrange("(p t) j -> p t j", t=PACK)
+        pos_sb = [sb("pos%d" % h, [P, PACK, HALF], F32) for h in range(HALVES)]
+        mix = sb("mix", [P, HALVES, D], F32)
+        w_raw = [sb("w_raw%d" % o, [P, PACK, H], F32) for o in range(PASSES)]
+        x_window = [sb("x_window%d" % o, [P, T], U32) for o in range(PASSES)]
+        q_raw = sb("q_raw", [P, PACK, R], F32)
+
+        nc.sync.dma_start(out=pos_sb[0][:], in_=pos_view[:, :, 0:HALF])
+        nc.sync.dma_start(out=mix[:], in_=mixw[0, :].rearrange("(h v d) -> v h d", h=HALVES, d=D))
+        nc.sync.dma_start(offsets[:], offs)
+        nc.sync.dma_start(out=pos_sb[1][:], in_=pos_view[:, :, HALF:S])
+        for o in range(PASSES):
+            rows = w1[o * K_PASS : (o + 1) * K_PASS, :]
+            nc.sync.dma_start(out=w_raw[o][:], in_=rows.rearrange("(p j) c -> p j c", j=PACK))
+        for o in range(PASSES):
+            words = x_words[o].rearrange("p n t -> p (n t)").bitcast(I32)
+            nc.sync.dma_start(out=x_window[o][:].bitcast(I32), in_=words)
+        nc.sync.dma_start(out=q_raw[:], in_=qT.rearrange("(p j) c -> p j c", j=PACK))
+        for quad in range(4):
+            for o in range(PASSES):
+                first = 32 * quad + 4 * o
+                nc.scalar.dma_start(
+                    out=scale_window[first : first + 4, :].bitcast(I32),
+                    in_=x_scales[o, 4 * quad : 4 * quad + 4, :].bitcast(I32),
+                )
+
+        pos_sum = []
+        for h in range(HALVES):
+            running = None
+            for d in range(D):
+                turned = bank(D * h + d, [P, PACK, P])
+                for t in range(PACK):
+                    nc.tensor.transpose(turned[:, t, :], pos_sb[h][:, t, d:HALF:D], ident[:])
+                total = sb("pos_sum%d_%d" % (h, d), [P, H], F32)
+                flat = turned[:].rearrange("v t p -> v (t p)")
+                weight = mix[:, h, d : d + 1]
+                if running is None:
+                    nc.vector.tensor_scalar(
+                        out=total[:], in0=flat, scalar1=weight, scalar2=None, op0=ALU.mult
+                    )
+                else:
+                    nc.vector.scalar_tensor_tensor(
+                        out=total[:], in0=flat, scalar=weight, in1=running[:],
+                        op0=ALU.mult, op1=ALU.add,
+                    )
+                running = total
+            pos_sum.append(running)
+
+        scale_picked = sb("scale_picked", [P, S], U8)
+        nc.vector.tensor_copy(out=scale_picked[:], in_=scale_window[:].indirect(offsets[:]))
+        x_scale = sb("x_scale", [P, S], U8)
+        nc.vector.tensor_copy(
+            out=x_scale[:].rearrange("p (h d v) -> p h d v", h=HALVES, d=D),
+            in_=scale_picked[:].rearrange("p (h v d) -> p h d v", h=HALVES, d=D),
+        )
+
+        w_codes, w_scale = [], []
+        for o in range(PASSES):
+            grouped = sb("w_grouped%d" % o, [P, H * PACK], BF16)
+            nc.scalar.copy(
+                out=grouped[:].rearrange("p (c i j) -> p c j i", i=4, j=PACK),
+                in_=w_raw[o][:].rearrange("p j (c i) -> p c j i", i=4),
+            )
+            codes = sb("w_codes%d" % o, [P, H], U32)
+            scale = sb("w_scale%d" % o, [P, H], U8)
+            nc.vector.quantize_mx(out=codes[:].bitcast(FP8X4), scales=scale[:], in_=grouped[:])
+            w_codes.append(codes)
+            w_scale.append(scale)
+
+        proj = [[bank(D * h + d, [P, H]) for d in range(D)] for h in range(HALVES)]
+        for o in range(PASSES):
+            for h in range(HALVES):
+                picked = sb("x_picked%d_%d" % (o, h), [P, HALF], U32)
+                cols = slice(h * HALF // 16, (h + 1) * HALF // 16)
+                nc.vector.tensor_copy(
+                    out=picked[:].rearrange("p (d v) -> p v d", d=D),
+                    in_=x_window[o][:].indirect(offsets[:, cols]),
+                )
+                for d in range(D):
+                    first = h * HALF + d * P
+                    nc.tensor.matmul_mx(
+                        out=proj[h][d][:],
+                        lhsT=picked[:, d * P : (d + 1) * P].bitcast(FP8X4),
+                        lhsT_scale=x_scale[4 * o : P, first : first + P],
+                        rhs=w_codes[o][:].bitcast(FP8X4),
+                        rhs_scale=w_scale[o][:],
+                        start=(o == 0),
+                        stop=(o == PASSES - 1),
+                    )
+
+        q_grouped = sb("q_grouped", [P, R * PACK], BF16)
+        nc.gpsimd.tensor_scalar(
+            out=q_grouped[:].rearrange("p (c j) -> p c j", j=PACK),
+            in0=q_raw[:].rearrange("p j c -> p c j"),
+            scalar1=1.0, scalar2=0.0, op0=ALU.mult, op1=ALU.add,
+        )
+
+        k_codes, k_scale = [], []
+        for h in range(HALVES):
+            parts = []
+            running = pos_sum[h]
+            for d in range(D):
+                part = sb("part%d_%d" % (h, d), [P, PACK, P], F32)
+                source = proj[h][d][:].rearrange("v (p t) -> v t p", t=PACK)
+                weight = mix[:, h, d : d + 1]
+                if d % 2 == 0:
+                    nc.scalar.activation(out=part[:], in_=source, func=ACT.Copy, scale=weight)
+                    parts.append(part)
+                else:
+                    prior = running[:] if d > 1 else running[:].rearrange("v (t p) -> v t p", t=PACK)
+                    nc.vector.scalar_tensor_tensor(
+                        out=part[:], in0=source, scalar=weight, in1=prior,
+                        op0=ALU.mult, op1=ALU.add,
+                    )
+                    running = part
+            parts.append(running)
+            if h == HALVES - 1:
+                q_codes = sb("q_codes", [P, R], U32, tag="part%d_1" % h)
+                q_scale = sb("q_scale", [P, R], U8)
+                nc.vector.quantize_mx(out=q_codes[:].bitcast(FP8X4), scales=q_scale[:], in_=q_grouped[:])
+            keys = bank(h, [P, PACK, P])
+            for n, part in enumerate(parts):
+                for t in range(PACK):
+                    nc.tensor.matmul(
+                        out=keys[:, t, :], lhsT=part[:, t, :], rhs=ident[:], is_transpose=True,
+                        start=(n == 0 and t == 0),
+                        stop=(n == len(parts) - 1 and t == PACK - 1),
+                    )
+            grouped = sb("k_grouped%d" % h, [P, P * PACK], BF16)
+            nc.scalar.copy(
+                out=grouped[:].rearrange("p (v t) -> p v t", t=PACK),
+                in_=keys[:].rearrange("p t v -> p v t"),
+            )
+            codes = sb("k_codes%d" % h, [P, P], U32)
+            scale = sb("k_scale%d" % h, [P, P], U8)
+            nc.vector.quantize_mx(out=codes[:].bitcast(FP8X4), scales=scale[:], in_=grouped[:])
+            k_codes.append(codes)
+            k_scale.append(scale)
+
+        scores = [bank(2 + n, [P, V]) for n in range(QTILES)]
+        for h in range(HALVES):
+            for n in range(QTILES):
+                nc.tensor.matmul_mx(
+                    out=scores[n][:, h * P : (h + 1) * P],
+                    lhsT=q_codes[:, n * P : (n + 1) * P].bitcast(FP8X4),
+                    lhsT_scale=q_scale[:, n * P : (n + 1) * P],
+                    rhs=k_codes[h][:].bitcast(FP8X4),
+                    rhs_scale=k_scale[h][:],
+                    start=True,
+                    stop=True,
+                )
+        for n in range(QTILES):
+            neg_max = sb("neg_max%d" % n, [P, 1], F32)
+            nc.vector.tensor_reduce(out=neg_max[:], in_=scores[n][:], axis=AX.X, op=ALU.max, negate=True)
+            ex = sb("ex%d" % n, [P, V], F32)
+            total = sb("total%d" % n, [P, 1], F32)
+            nc.scalar.activation(
+                out=ex[:], in_=scores[n][:], func=ACT.Exp, bias=neg_max[:], accum_out=total[:]
+            )
+            inverse = sb("inverse%d" % n, [P, 1], F32)
+            nc.vector.reciprocal(out=inverse[:], in_=total[:])
+            weights = sb("weights%d" % n, [P, V], F32)
+            nc.vector.tensor_scalar(
+                out=weights[:], in0=ex[:], scalar1=inverse[:], scalar2=None, op0=ALU.mult
+            )
+            nc.sync.dma_start(out=out[n * P : (n + 1) * P, :], in_=weights[:])

@@ -61,10 +61,20 @@ def tile_picked_ycblk_wts_p_kernel(
         x_window = [sb("x_window%d" % o, [P, T], U32) for o in range(PASSES)]
         q_raw = sb("q_raw", [P, PACK, R], F32)
 
+        def load_scale_rows(o):
+            for quad in range(4):
+                first = 32 * quad + 4 * o
+                nc.sync.dma_start(
+                    out=scale_window[first : first + 4, :].bitcast(I32),
+                    in_=x_scales[o, 4 * quad : 4 * quad + 4, :].bitcast(I32),
+                )
+
         nc.sync.dma_start(out=pos_sb[0][:], in_=pos_view[:, :, 0:HALF])
         nc.sync.dma_start(out=mix[:], in_=mixw[0, :].rearrange("(h v d) -> v h d", h=HALVES, d=D))
         nc.sync.dma_start(offsets[:], offs)
+        load_scale_rows(0)
         nc.sync.dma_start(out=pos_sb[1][:], in_=pos_view[:, :, HALF:S])
+        load_scale_rows(1)
         for o in range(PASSES):
             rows = w1[o * K_PASS : (o + 1) * K_PASS, :]
             nc.sync.dma_start(out=w_raw[o][:], in_=rows.rearrange("(p j) c -> p j c", j=PACK))
@@ -72,13 +82,6 @@ def tile_picked_ycblk_wts_p_kernel(
             words = x_words[o].rearrange("p n t -> p (n t)").bitcast(I32)
             nc.sync.dma_start(out=x_window[o][:].bitcast(I32), in_=words)
         nc.sync.dma_start(out=q_raw[:], in_=qT.rearrange("(p j) c -> p j c", j=PACK))
-        for quad in range(4):
-            for o in range(PASSES):
-                first = 32 * quad + 4 * o
-                nc.scalar.dma_start(
-                    out=scale_window[first : first + 4, :].bitcast(I32),
-                    in_=x_scales[o, 4 * quad : 4 * quad + 4, :].bitcast(I32),
-                )
 
         pos_sum = []
         for h in range(HALVES):
@@ -87,13 +90,11 @@ def tile_picked_ycblk_wts_p_kernel(
                 turned = bank(D * h + d, [P, PACK, P])
                 for t in range(PACK):
                     nc.tensor.transpose(turned[:, t, :], pos_sb[h][:, t, d:HALF:D], ident[:])
-                total = sb("pos_sum%d_%d" % (h, d), [P, H], F32)
+                total = sb("pos_sum%d_%d" % (h, d), [P, H], F32, tag="pos_sum0_2" if (h, d) == (1, 1) else None)
                 flat = turned[:].rearrange("v t p -> v (t p)")
                 weight = mix[:, h, d : d + 1]
                 if running is None:
-                    nc.vector.tensor_scalar(
-                        out=total[:], in0=flat, scalar1=weight, scalar2=None, op0=ALU.mult
-                    )
+                    nc.scalar.activation(out=total[:], in_=flat, func=ACT.Copy, scale=weight)
                 else:
                     nc.vector.scalar_tensor_tensor(
                         out=total[:], in0=flat, scalar=weight, in1=running[:],
@@ -101,14 +102,15 @@ def tile_picked_ycblk_wts_p_kernel(
                     )
                 running = total
             pos_sum.append(running)
+            if h == 0:
+                scale_picked = sb("scale_picked", [P, S], U8, tag="pos_sum0_2")
+                nc.vector.tensor_copy(out=scale_picked[:], in_=scale_window[:].indirect(offsets[:]))
+                x_scale = sb("x_scale", [P, S], U8)
+                nc.vector.tensor_copy(
+                    out=x_scale[:].rearrange("p (h d v) -> p h d v", h=HALVES, d=D),
+                    in_=scale_picked[:].rearrange("p (h v d) -> p h d v", h=HALVES, d=D),
+                )
 
-        scale_picked = sb("scale_picked", [P, S], U8)
-        nc.vector.tensor_copy(out=scale_picked[:], in_=scale_window[:].indirect(offsets[:]))
-        x_scale = sb("x_scale", [P, S], U8)
-        nc.vector.tensor_copy(
-            out=x_scale[:].rearrange("p (h d v) -> p h d v", h=HALVES, d=D),
-            in_=scale_picked[:].rearrange("p (h v d) -> p h d v", h=HALVES, d=D),
-        )
 
         w_codes, w_scale = [], []
         for o in range(PASSES):
@@ -117,7 +119,7 @@ def tile_picked_ycblk_wts_p_kernel(
                 out=grouped[:].rearrange("p (c i j) -> p c j i", i=4, j=PACK),
                 in_=w_raw[o][:].rearrange("p j (c i) -> p c j i", i=4),
             )
-            codes = sb("w_codes%d" % o, [P, H], U32)
+            codes = sb("w_codes%d" % o, [P, H], U32, tag="pos_sum1_2" if o == 0 else None)
             scale = sb("w_scale%d" % o, [P, H], U8)
             nc.vector.quantize_mx(out=codes[:].bitcast(FP8X4), scales=scale[:], in_=grouped[:])
             w_codes.append(codes)
@@ -126,7 +128,8 @@ def tile_picked_ycblk_wts_p_kernel(
         proj = [[bank(D * h + d, [P, H]) for d in range(D)] for h in range(HALVES)]
         for o in range(PASSES):
             for h in range(HALVES):
-                picked = sb("x_picked%d_%d" % (o, h), [P, HALF], U32)
+                tag = [["w_grouped1", "w_raw1"], ["x_window0", "w_scale0"]][o][h]
+                picked = sb("x_picked%d_%d" % (o, h), [P, HALF], U32, tag=tag)
                 cols = slice(h * HALF // 16, (h + 1) * HALF // 16)
                 nc.vector.tensor_copy(
                     out=picked[:].rearrange("p (d v) -> p v d", d=D),
@@ -153,25 +156,22 @@ def tile_picked_ycblk_wts_p_kernel(
 
         k_codes, k_scale = [], []
         for h in range(HALVES):
-            parts = []
-            running = pos_sum[h]
+            parts = [pos_sum[h][:].rearrange("v (t p) -> v t p", t=PACK)]
             for d in range(D):
                 part = sb("part%d_%d" % (h, d), [P, PACK, P], F32)
                 source = proj[h][d][:].rearrange("v (p t) -> v t p", t=PACK)
                 weight = mix[:, h, d : d + 1]
                 if d % 2 == 0:
                     nc.scalar.activation(out=part[:], in_=source, func=ACT.Copy, scale=weight)
-                    parts.append(part)
+                    prior = part
                 else:
-                    prior = running[:] if d > 1 else running[:].rearrange("v (t p) -> v t p", t=PACK)
                     nc.vector.scalar_tensor_tensor(
-                        out=part[:], in0=source, scalar=weight, in1=prior,
+                        out=part[:], in0=source, scalar=weight, in1=prior[:],
                         op0=ALU.mult, op1=ALU.add,
                     )
-                    running = part
-            parts.append(running)
+                    parts.append(part[:])
             if h == HALVES - 1:
-                q_codes = sb("q_codes", [P, R], U32, tag="part%d_1" % h)
+                q_codes = sb("q_codes", [P, R], U32, tag="part%d_2" % h)
                 q_scale = sb("q_scale", [P, R], U8)
                 nc.vector.quantize_mx(out=q_codes[:].bitcast(FP8X4), scales=q_scale[:], in_=q_grouped[:])
             keys = bank(h, [P, PACK, P])
@@ -216,7 +216,8 @@ def tile_picked_ycblk_wts_p_kernel(
             inverse = sb("inverse%d" % n, [P, 1], F32)
             nc.vector.reciprocal(out=inverse[:], in_=total[:])
             weights = sb("weights%d" % n, [P, V], F32)
-            nc.vector.tensor_scalar(
-                out=weights[:], in0=ex[:], scalar1=inverse[:], scalar2=None, op0=ALU.mult
+            engine = nc.vector if n == QTILES - 1 else nc.gpsimd
+            engine.tensor_scalar(
+                out=weights[:], in0=ex[:], scalar1=inverse[:], scalar2=0.0, op0=ALU.mult, op1=ALU.add
             )
             nc.sync.dma_start(out=out[n * P : (n + 1) * P, :], in_=weights[:])

@@ -33,32 +33,36 @@ def tile_picked_ycblk_wts_p_kernel(
     nc = tc.nc
     with ExitStack() as ctx:
         keep = ctx.enter_context(tc.tile_pool(name="keep", bufs=1))
+        placed = ctx.enter_context(tc.tile_pool(name="placed", bufs=1))
         psum = ctx.enter_context(tc.psum_pool(name="psum", bufs=1))
 
         def sb(name, shape, dtype, tag=None):
             return keep.tile(shape, dtype, name=name, tag=tag or name, align_bytes=64)
+
+        def at(offset, name, shape, dtype):
+            return placed.tile(shape, dtype, name=name, offset=offset, align_bytes=64)
 
         def bank(index, shape):
             return psum.tile(shape, F32, name="bank%d" % index, tag="bank%d" % index)
 
         offsets = keep.tile([P, S // 16], U16, name="offsets")
 
+        scale_window = sb("scale_window", [P, T], U8)
+        nc.vector.memset(scale_window[:].bitcast(I32), 0)
         warm_in = sb("warm_in", [P, 1], F32)
         warm_out = sb("warm_out", [P, 1], F32)
-        nc.vector.memset(warm_in[:], 0.0)
+        nc.gpsimd.memset(warm_in[:], 0.0)
         nc.scalar.activation(out=warm_out[:], in_=warm_in[:], func=ACT.Exp)
 
         ident = sb("ident", [P, P], F32)
         make_identity(nc, ident[:])
 
-        scale_window = sb("scale_window", [P, T], U8)
-        nc.vector.memset(scale_window[:].bitcast(I32), 0)
 
         pos_view = pos.rearrange("(p t) j -> p t j", t=PACK)
         pos_sb = [sb("pos%d" % h, [P, PACK, HALF], F32) for h in range(HALVES)]
         mix = sb("mix", [P, HALVES, D], F32)
         w_raw = [sb("w_raw%d" % o, [P, PACK, H], F32) for o in range(PASSES)]
-        x_window = [sb("x_window%d" % o, [P, T], U32) for o in range(PASSES)]
+        x_window = [at(0, "x_window0", [P, T], U32), sb("x_window1", [P, T], U32)]
         q_raw = sb("q_raw", [P, PACK, R], F32)
 
         def load_scale_rows(o):
@@ -83,53 +87,65 @@ def tile_picked_ycblk_wts_p_kernel(
             nc.sync.dma_start(out=x_window[o][:].bitcast(I32), in_=words)
         nc.sync.dma_start(out=q_raw[:], in_=qT.rearrange("(p j) c -> p j c", j=PACK))
 
-        pos_sum = []
+        pos_dealt = []
         for h in range(HALVES):
-            running = None
+            if h == 0:
+                dealt = sb("pos_dealt0", [P, D, PACK * P], F32)
+            else:
+                dealt = at(4 * T, "pos_dealt1", [P, D, PACK * P], F32)
+            nc.vector.tensor_copy(
+                out=dealt[:].rearrange("p d n -> p n d"),
+                in_=pos_sb[h][:].rearrange("p t (v d) -> p (t v) d", d=D),
+            )
+            pos_dealt.append(dealt)
+        scale_picked = sb("scale_picked", [P, S], U8, tag="pos1")
+        nc.vector.tensor_copy(out=scale_picked[:], in_=scale_window[:].indirect(offsets[:]))
+        x_scale = sb("x_scale", [P, S], U8)
+        nc.vector.tensor_copy(
+            out=x_scale[:].rearrange("p (h d v) -> p h d v", h=HALVES, d=D),
+            in_=scale_picked[:].rearrange("p (h v d) -> p h d v", h=HALVES, d=D),
+        )
+        turned = [[bank(D * h + d, [P, H]) for d in range(D)] for h in range(HALVES)]
+        for h in range(HALVES):
             for d in range(D):
-                turned = bank(D * h + d, [P, PACK, P])
                 for t in range(PACK):
-                    nc.tensor.transpose(turned[:, t, :], pos_sb[h][:, t, d:HALF:D], ident[:])
-                total = sb("pos_sum%d_%d" % (h, d), [P, H], F32, tag="pos_sum0_2" if (h, d) == (1, 1) else None)
-                flat = turned[:].rearrange("v t p -> v (t p)")
+                    cols = slice(t * P, (t + 1) * P)
+                    nc.tensor.transpose(turned[h][d][:, cols], pos_dealt[h][:, d, cols], ident[:])
+        pos_sum = [None] * HALVES
+        for d in range(D):
+            for h in range(HALVES):
+                tag = ["pos1", "pos_sum0_0"][h] if d == 1 else None
+                total = sb("pos_sum%d_%d" % (h, d), [P, H], F32, tag=tag)
                 weight = mix[:, h, d : d + 1]
-                if running is None:
-                    nc.scalar.activation(out=total[:], in_=flat, func=ACT.Copy, scale=weight)
+                if d == 0:
+                    nc.scalar.activation(out=total[:], in_=turned[h][d][:], func=ACT.Copy, scale=weight)
                 else:
                     nc.vector.scalar_tensor_tensor(
-                        out=total[:], in0=flat, scalar=weight, in1=running[:],
+                        out=total[:], in0=turned[h][d][:], scalar=weight, in1=pos_sum[h][:],
                         op0=ALU.mult, op1=ALU.add,
                     )
-                running = total
-            pos_sum.append(running)
-            if h == 0:
-                scale_picked = sb("scale_picked", [P, S], U8, tag="pos_sum0_2")
-                nc.vector.tensor_copy(out=scale_picked[:], in_=scale_window[:].indirect(offsets[:]))
-                x_scale = sb("x_scale", [P, S], U8)
-                nc.vector.tensor_copy(
-                    out=x_scale[:].rearrange("p (h d v) -> p h d v", h=HALVES, d=D),
-                    in_=scale_picked[:].rearrange("p (h v d) -> p h d v", h=HALVES, d=D),
-                )
+                pos_sum[h] = total
 
-
-        w_codes, w_scale = [], []
+        w_grouped = []
         for o in range(PASSES):
-            grouped = sb("w_grouped%d" % o, [P, H * PACK], BF16)
+            grouped = at(4 * T + o * 2 * H * PACK, "w_grouped%d" % o, [P, H * PACK], BF16)
             nc.scalar.copy(
                 out=grouped[:].rearrange("p (c i j) -> p c j i", i=4, j=PACK),
                 in_=w_raw[o][:].rearrange("p j (c i) -> p c j i", i=4),
             )
-            codes = sb("w_codes%d" % o, [P, H], U32, tag="pos_sum1_2" if o == 0 else None)
-            scale = sb("w_scale%d" % o, [P, H], U8)
-            nc.vector.quantize_mx(out=codes[:].bitcast(FP8X4), scales=scale[:], in_=grouped[:])
-            w_codes.append(codes)
-            w_scale.append(scale)
+            w_grouped.append(grouped)
 
         proj = [[bank(D * h + d, [P, H]) for d in range(D)] for h in range(HALVES)]
         for o in range(PASSES):
+            if o == 0:
+                w_codes = sb("w_codes0", [P, H], U32, tag="pos_sum1_2")
+            else:
+                w_codes = at(4 * S, "w_codes1", [P, H], U32)
+            w_scale = sb("w_scale%d" % o, [P, H], U8)
+            nc.vector.quantize_mx(out=w_codes[:].bitcast(FP8X4), scales=w_scale[:], in_=w_grouped[o][:])
             for h in range(HALVES):
-                tag = [["w_grouped1", "w_raw1"], ["x_window0", "w_scale0"]][o][h]
-                picked = sb("x_picked%d_%d" % (o, h), [P, HALF], U32, tag=tag)
+                base = 4 * T if o == 0 else 0
+                picked = at(base + 4 * HALF * h, "x_picked%d_%d" % (o, h), [P, HALF], U32)
                 cols = slice(h * HALF // 16, (h + 1) * HALF // 16)
                 nc.vector.tensor_copy(
                     out=picked[:].rearrange("p (d v) -> p v d", d=D),
@@ -141,8 +157,8 @@ def tile_picked_ycblk_wts_p_kernel(
                         out=proj[h][d][:],
                         lhsT=picked[:, d * P : (d + 1) * P].bitcast(FP8X4),
                         lhsT_scale=x_scale[4 * o : P, first : first + P],
-                        rhs=w_codes[o][:].bitcast(FP8X4),
-                        rhs_scale=w_scale[o][:],
+                        rhs=w_codes[:].bitcast(FP8X4),
+                        rhs_scale=w_scale[:],
                         start=(o == 0),
                         stop=(o == PASSES - 1),
                     )
@@ -216,8 +232,7 @@ def tile_picked_ycblk_wts_p_kernel(
             inverse = sb("inverse%d" % n, [P, 1], F32)
             nc.vector.reciprocal(out=inverse[:], in_=total[:])
             weights = sb("weights%d" % n, [P, V], F32)
-            engine = nc.vector if n == QTILES - 1 else nc.gpsimd
-            engine.tensor_scalar(
-                out=weights[:], in0=ex[:], scalar1=inverse[:], scalar2=0.0, op0=ALU.mult, op1=ALU.add
+            nc.vector.tensor_scalar(
+                out=weights[:], in0=ex[:], scalar1=inverse[:], scalar2=None, op0=ALU.mult
             )
             nc.sync.dma_start(out=out[n * P : (n + 1) * P, :], in_=weights[:])

@@ -25,6 +25,7 @@ PASSES = K // K_PASS
 HALVES = V // P
 HALF = S // HALVES
 QTILES = R // P
+SHARE = H // 2
 
 
 def tile_picked_ycblk_wts_p_kernel(
@@ -59,10 +60,11 @@ def tile_picked_ycblk_wts_p_kernel(
 
 
         pos_view = pos.rearrange("(p t) j -> p t j", t=PACK)
-        pos_sb = [sb("pos%d" % h, [P, PACK, HALF], F32) for h in range(HALVES)]
+        pos_sb = [[sb("pos%d_%d" % (h, g), [P, 2, HALF], F32) for g in range(2)] for h in range(HALVES)]
         mix = sb("mix", [P, HALVES, D], F32)
-        w_raw = [sb("w_raw%d" % o, [P, PACK, H], F32) for o in range(PASSES)]
-        x_window = [at(0, "x_window0", [P, T], U32), sb("x_window1", [P, T], U32)]
+        w_first = sb("w_first", [P, PACK, H], F32)
+        w_last = [sb("w_last%d" % n, [P, PACK, SHARE], F32) for n in range(2)]
+        x_window = [at(4 * T, "x_window0", [P, T], U32), sb("x_window1", [P, T], U32)]
         q_raw = sb("q_raw", [P, PACK, R], F32)
 
         def load_scale_rows(o):
@@ -73,130 +75,160 @@ def tile_picked_ycblk_wts_p_kernel(
                     in_=x_scales[o, 4 * quad : 4 * quad + 4, :].bitcast(I32),
                 )
 
-        nc.sync.dma_start(out=pos_sb[0][:], in_=pos_view[:, :, 0:HALF])
+        def load_pos(h, g):
+            nc.sync.dma_start(out=pos_sb[h][g][:], in_=pos_view[:, 2 * g : 2 * g + 2, h * HALF : (h + 1) * HALF])
+
+        def load_weights(tile, o, first, last):
+            rows = w1[o * K_PASS : (o + 1) * K_PASS, first:last]
+            nc.sync.dma_start(out=tile[:], in_=rows.rearrange("(p j) c -> p j c", j=PACK))
+
+        load_pos(0, 0)
         nc.sync.dma_start(out=mix[:], in_=mixw[0, :].rearrange("(h v d) -> v h d", h=HALVES, d=D))
         nc.sync.dma_start(offsets[:], offs)
+        load_pos(0, 1)
+        load_pos(1, 0)
+        load_pos(1, 1)
         load_scale_rows(0)
-        nc.sync.dma_start(out=pos_sb[1][:], in_=pos_view[:, :, HALF:S])
+        load_weights(w_first, 0, 0, H)
         load_scale_rows(1)
-        for o in range(PASSES):
-            rows = w1[o * K_PASS : (o + 1) * K_PASS, :]
-            nc.sync.dma_start(out=w_raw[o][:], in_=rows.rearrange("(p j) c -> p j c", j=PACK))
         for o in range(PASSES):
             words = x_words[o].rearrange("p n t -> p (n t)").bitcast(I32)
             nc.sync.dma_start(out=x_window[o][:].bitcast(I32), in_=words)
+        for n in range(2):
+            load_weights(w_last[n], 1, n * SHARE, (n + 1) * SHARE)
         nc.sync.dma_start(out=q_raw[:], in_=qT.rearrange("(p j) c -> p j c", j=PACK))
 
-        pos_dealt = []
-        for h in range(HALVES):
-            if h == 0:
-                dealt = sb("pos_dealt0", [P, D, PACK * P], F32)
-            else:
-                dealt = at(4 * T, "pos_dealt1", [P, D, PACK * P], F32)
+        turned = [[bank(D * h + d, [P, H]) for d in range(D)] for h in range(HALVES)]
+
+        def turn_positions(h, g, tag):
+            dealt = sb("pos_dealt%d_%d" % (h, g), [P, D, 2 * P], F32, tag=tag)
             nc.vector.tensor_copy(
                 out=dealt[:].rearrange("p d n -> p n d"),
-                in_=pos_sb[h][:].rearrange("p t (v d) -> p (t v) d", d=D),
+                in_=pos_sb[h][g][:].rearrange("p t (v d) -> p (t v) d", d=D),
             )
-            pos_dealt.append(dealt)
-        scale_picked = sb("scale_picked", [P, S], U8, tag="pos1")
+            for d in range(D):
+                for t in range(2):
+                    cols = slice((2 * g + t) * P, (2 * g + t + 1) * P)
+                    nc.tensor.transpose(turned[h][d][:, cols], dealt[:, d, t * P : (t + 1) * P], ident[:])
+
+        def weigh(total, source, h, d, prior):
+            weight = mix[:, h, d : d + 1]
+            if prior is None:
+                nc.scalar.activation(out=total[:], in_=source, func=ACT.Copy, scale=weight)
+            else:
+                nc.vector.scalar_tensor_tensor(
+                    out=total[:], in0=source, scalar=weight, in1=prior[:], op0=ALU.mult, op1=ALU.add
+                )
+            return total
+
+        def add_position(h, d, total, prior):
+            return weigh(total, turned[h][d][:].rearrange("v (t p) -> v t p", t=PACK), h, d, prior)
+
+        def cast_weights(grouped, raw):
+            nc.scalar.copy(
+                out=grouped[:].rearrange("p (c i j) -> p c j i", i=4, j=PACK),
+                in_=raw[:].rearrange("p j (c i) -> p c j i", i=4),
+            )
+
+        def gather_words(o, h, picked):
+            cols = slice(h * HALF // 16, (h + 1) * HALF // 16)
+            nc.vector.tensor_copy(
+                out=picked[:].rearrange("p (d v) -> p v d", d=D),
+                in_=x_window[o][:].indirect(offsets[:, cols]),
+            )
+            return picked
+
+        shape = [P, PACK, P]
+        pos_sum = []
+        for h in range(HALVES):
+            for g in range(2):
+                turn_positions(h, g, None)
+        for h in range(HALVES):
+            pairs = []
+            for d in (0, 2):
+                name = "pos_term%d_%d" % (h, d)
+                tile = at(4 * S * d, name, shape, F32) if h == 1 else sb(name, shape, F32)
+                term = add_position(h, d, tile, None)
+                pairs.append(add_position(h, d + 1, sb("pos_pair%d_%d" % (h, d), shape, F32), term))
+            total = sb("pos_sum%d" % h, shape, F32)
+            nc.gpsimd.tensor_tensor(out=total[:], in0=pairs[0][:], in1=pairs[1][:], op=ALU.add)
+            pos_sum.append(total)
+        scale_picked = at(8 * S + HALF, "scale_picked", [P, S], U8)
         nc.vector.tensor_copy(out=scale_picked[:], in_=scale_window[:].indirect(offsets[:]))
         x_scale = sb("x_scale", [P, S], U8)
         nc.vector.tensor_copy(
             out=x_scale[:].rearrange("p (h d v) -> p h d v", h=HALVES, d=D),
             in_=scale_picked[:].rearrange("p (h v d) -> p h d v", h=HALVES, d=D),
         )
-        turned = [[bank(D * h + d, [P, H]) for d in range(D)] for h in range(HALVES)]
-        for h in range(HALVES):
-            for d in range(D):
-                for t in range(PACK):
-                    cols = slice(t * P, (t + 1) * P)
-                    nc.tensor.transpose(turned[h][d][:, cols], pos_dealt[h][:, d, cols], ident[:])
-        pos_sum = [None] * HALVES
-        for d in range(D):
-            for h in range(HALVES):
-                tag = ["pos1", "pos_sum0_0"][h] if d == 1 else None
-                total = sb("pos_sum%d_%d" % (h, d), [P, H], F32, tag=tag)
-                weight = mix[:, h, d : d + 1]
-                if d == 0:
-                    nc.scalar.activation(out=total[:], in_=turned[h][d][:], func=ACT.Copy, scale=weight)
-                else:
-                    nc.vector.scalar_tensor_tensor(
-                        out=total[:], in0=turned[h][d][:], scalar=weight, in1=pos_sum[h][:],
-                        op0=ALU.mult, op1=ALU.add,
-                    )
-                pos_sum[h] = total
 
-        w_grouped = []
-        for o in range(PASSES):
-            grouped = at(4 * T + o * 2 * H * PACK, "w_grouped%d" % o, [P, H * PACK], BF16)
-            nc.scalar.copy(
-                out=grouped[:].rearrange("p (c i j) -> p c j i", i=4, j=PACK),
-                in_=w_raw[o][:].rearrange("p j (c i) -> p c j i", i=4),
+        w_scale = [sb("w_scale%d" % o, [P, H], U8) for o in range(PASSES)]
+        grouped = at(0, "w_grouped0", [P, H * PACK], BF16)
+        cast_weights(grouped, w_first)
+        w_codes = [at(8 * S, "w_codes0", [P, H], U32)]
+        nc.vector.quantize_mx(out=w_codes[0][:].bitcast(FP8X4), scales=w_scale[0][:], in_=grouped[:])
+        picked = [
+            [gather_words(0, h, at(4 * HALF * h, "x_picked0_%d" % h, [P, HALF], U32)) for h in range(HALVES)]
+        ]
+
+        def product(o, h, d, cols, start, stop):
+            first = h * HALF + d * P
+            nc.tensor.matmul_mx(
+                out=proj[h][d][:, cols],
+                lhsT=picked[o][h][:, d * P : (d + 1) * P].bitcast(FP8X4),
+                lhsT_scale=x_scale[4 * o : P, first : first + P],
+                rhs=w_codes[o][:, cols].bitcast(FP8X4),
+                rhs_scale=w_scale[o][:, cols],
+                start=start,
+                stop=stop,
             )
-            w_grouped.append(grouped)
 
         proj = [[bank(D * h + d, [P, H]) for d in range(D)] for h in range(HALVES)]
-        for o in range(PASSES):
-            if o == 0:
-                w_codes = sb("w_codes0", [P, H], U32, tag="pos_sum1_2")
-            else:
-                w_codes = at(4 * S, "w_codes1", [P, H], U32)
-            w_scale = sb("w_scale%d" % o, [P, H], U8)
-            nc.vector.quantize_mx(out=w_codes[:].bitcast(FP8X4), scales=w_scale[:], in_=w_grouped[o][:])
-            for h in range(HALVES):
-                base = 4 * T if o == 0 else 0
-                picked = at(base + 4 * HALF * h, "x_picked%d_%d" % (o, h), [P, HALF], U32)
-                cols = slice(h * HALF // 16, (h + 1) * HALF // 16)
-                nc.vector.tensor_copy(
-                    out=picked[:].rearrange("p (d v) -> p v d", d=D),
-                    in_=x_window[o][:].indirect(offsets[:, cols]),
-                )
-                for d in range(D):
-                    first = h * HALF + d * P
-                    nc.tensor.matmul_mx(
-                        out=proj[h][d][:],
-                        lhsT=picked[:, d * P : (d + 1) * P].bitcast(FP8X4),
-                        lhsT_scale=x_scale[4 * o : P, first : first + P],
-                        rhs=w_codes[:].bitcast(FP8X4),
-                        rhs_scale=w_scale[:],
-                        start=(o == 0),
-                        stop=(o == PASSES - 1),
-                    )
+        for h in range(HALVES):
+            for d in range(D):
+                product(0, h, d, slice(0, H), True, False)
 
-        q_grouped = sb("q_grouped", [P, R * PACK], BF16)
+        picked.append(
+            [gather_words(1, h, at(4 * T + 4 * HALF * h, "x_picked1_%d" % h, [P, HALF], U32)) for h in range(HALVES)]
+        )
+        tiles = [(h, d) for h in range(HALVES) for d in range(D)]
+        w_codes.append(sb("w_codes1", [P, H], U32, tag="x_window1"))
+        for n in range(2):
+            grouped = sb("w_grouped1_%d" % n, [P, SHARE * PACK], BF16, tag=["w_first", "w_last0"][n])
+            cast_weights(grouped, w_last[n])
+            cols = slice(n * SHARE, (n + 1) * SHARE)
+            nc.vector.quantize_mx(out=w_codes[1][:, cols].bitcast(FP8X4), scales=w_scale[1][:, cols], in_=grouped[:])
+            for h, d in tiles[:6]:
+                product(1, h, d, cols, False, n == 1)
+        for h, d in tiles[6:]:
+            product(1, h, d, slice(0, H), False, True)
+
+        q_grouped = sb("q_grouped", [P, R * PACK], BF16, tag="w_last0")
         nc.gpsimd.tensor_scalar(
             out=q_grouped[:].rearrange("p (c j) -> p c j", j=PACK),
             in0=q_raw[:].rearrange("p j c -> p c j"),
             scalar1=1.0, scalar2=0.0, op0=ALU.mult, op1=ALU.add,
         )
 
+        parts = []
+        for h in range(HALVES):
+            part = {}
+            for d in range(D):
+                prior = {0: None, 1: pos_sum[h], 2: None, 3: part.get(0)}[d]
+                source = proj[h][d][:].rearrange("v (p t) -> v t p", t=PACK)
+                part[d] = weigh(sb("part%d_%d" % (h, d), shape, F32), source, h, d, prior)
+            parts.append([part[1], part[2], part[3]])
+        q_codes = sb("q_codes", [P, R], U32, tag="part1_0")
+        q_scale = sb("q_scale", [P, R], U8)
+        nc.vector.quantize_mx(out=q_codes[:].bitcast(FP8X4), scales=q_scale[:], in_=q_grouped[:])
         k_codes, k_scale = [], []
         for h in range(HALVES):
-            parts = [pos_sum[h][:].rearrange("v (t p) -> v t p", t=PACK)]
-            for d in range(D):
-                part = sb("part%d_%d" % (h, d), [P, PACK, P], F32)
-                source = proj[h][d][:].rearrange("v (p t) -> v t p", t=PACK)
-                weight = mix[:, h, d : d + 1]
-                if d % 2 == 0:
-                    nc.scalar.activation(out=part[:], in_=source, func=ACT.Copy, scale=weight)
-                    prior = part
-                else:
-                    nc.vector.scalar_tensor_tensor(
-                        out=part[:], in0=source, scalar=weight, in1=prior[:],
-                        op0=ALU.mult, op1=ALU.add,
-                    )
-                    parts.append(part[:])
-            if h == HALVES - 1:
-                q_codes = sb("q_codes", [P, R], U32, tag="part%d_2" % h)
-                q_scale = sb("q_scale", [P, R], U8)
-                nc.vector.quantize_mx(out=q_codes[:].bitcast(FP8X4), scales=q_scale[:], in_=q_grouped[:])
-            keys = bank(h, [P, PACK, P])
-            for n, part in enumerate(parts):
+            keys = bank(h, shape)
+            for n, part in enumerate(parts[h]):
                 for t in range(PACK):
                     nc.tensor.matmul(
                         out=keys[:, t, :], lhsT=part[:, t, :], rhs=ident[:], is_transpose=True,
                         start=(n == 0 and t == 0),
-                        stop=(n == len(parts) - 1 and t == PACK - 1),
+                        stop=(n == len(parts[h]) - 1 and t == PACK - 1),
                     )
             grouped = sb("k_grouped%d" % h, [P, P * PACK], BF16)
             nc.scalar.copy(
@@ -209,7 +241,7 @@ def tile_picked_ycblk_wts_p_kernel(
             k_codes.append(codes)
             k_scale.append(scale)
 
-        scores = [bank(2 + n, [P, V]) for n in range(QTILES)]
+        scores = [bank(n, [P, V]) for n in (2, 3, 6, 7)]
         for h in range(HALVES):
             for n in range(QTILES):
                 nc.tensor.matmul_mx(
@@ -232,7 +264,10 @@ def tile_picked_ycblk_wts_p_kernel(
             inverse = sb("inverse%d" % n, [P, 1], F32)
             nc.vector.reciprocal(out=inverse[:], in_=total[:])
             weights = sb("weights%d" % n, [P, V], F32)
-            nc.vector.tensor_scalar(
-                out=weights[:], in0=ex[:], scalar1=inverse[:], scalar2=None, op0=ALU.mult
-            )
+            if n == QTILES - 2:
+                nc.scalar.activation(out=weights[:], in_=ex[:], func=ACT.Copy, scale=inverse[:])
+            else:
+                nc.vector.tensor_scalar(
+                    out=weights[:], in0=ex[:], scalar1=inverse[:], scalar2=None, op0=ALU.mult
+                )
             nc.sync.dma_start(out=out[n * P : (n + 1) * P, :], in_=weights[:])

@@ -49,7 +49,10 @@ def tile_picked_ycblk_wts_p_kernel(
         offsets = keep.tile([P, S // 16], U16, name="offsets")
 
         scale_window = sb("scale_window", [P, T], U8)
-        nc.vector.memset(scale_window[:].bitcast(I32), 0)
+        for first, last in ((32, 64), (64, P)):
+            nc.vector.memset(scale_window[first:last, :].bitcast(I32), 0)
+        x_scale = sb("x_scale", [P, S], U8)
+        nc.vector.memset(x_scale[:].bitcast(I32), 0)
         warm_in = sb("warm_in", [P, 1], F32)
         warm_out = sb("warm_out", [P, 1], F32)
         nc.gpsimd.memset(warm_in[:], 0.0)
@@ -67,14 +70,6 @@ def tile_picked_ycblk_wts_p_kernel(
         x_window = [at(4 * T, "x_window0", [P, T], U32), sb("x_window1", [P, T], U32)]
         q_raw = sb("q_raw", [P, PACK, R], F32)
 
-        def load_scale_rows(o):
-            for quad in range(4):
-                first = 32 * quad + 4 * o
-                nc.sync.dma_start(
-                    out=scale_window[first : first + 4, :].bitcast(I32),
-                    in_=x_scales[o, 4 * quad : 4 * quad + 4, :].bitcast(I32),
-                )
-
         def load_pos(h, g):
             nc.sync.dma_start(out=pos_sb[h][g][:], in_=pos_view[:, 2 * g : 2 * g + 2, h * HALF : (h + 1) * HALF])
 
@@ -82,15 +77,17 @@ def tile_picked_ycblk_wts_p_kernel(
             rows = w1[o * K_PASS : (o + 1) * K_PASS, first:last]
             nc.sync.dma_start(out=tile[:], in_=rows.rearrange("(p j) c -> p j c", j=PACK))
 
-        load_pos(0, 0)
-        nc.sync.dma_start(out=mix[:], in_=mixw[0, :].rearrange("(h v d) -> v h d", h=HALVES, d=D))
+        nc.sync.dma_start(
+            out=scale_window[0:32, :].bitcast(I32),
+            in_=x_scales.rearrange("o q n -> (o q) n").bitcast(I32),
+        )
         nc.sync.dma_start(offsets[:], offs)
+        load_pos(0, 0)
         load_pos(0, 1)
+        nc.sync.dma_start(out=mix[:], in_=mixw[0, :].rearrange("(h v d) -> v h d", h=HALVES, d=D))
         load_pos(1, 0)
         load_pos(1, 1)
-        load_scale_rows(0)
         load_weights(w_first, 0, 0, H)
-        load_scale_rows(1)
         for o in range(PASSES):
             words = x_words[o].rearrange("p n t -> p (n t)").bitcast(I32)
             nc.sync.dma_start(out=x_window[o][:].bitcast(I32), in_=words)
@@ -102,7 +99,8 @@ def tile_picked_ycblk_wts_p_kernel(
 
         def turn_positions(h, g, tag):
             dealt = sb("pos_dealt%d_%d" % (h, g), [P, D, 2 * P], F32, tag=tag)
-            nc.vector.tensor_copy(
+            copy = nc.scalar.copy if g == 0 else nc.vector.tensor_copy
+            copy(
                 out=dealt[:].rearrange("p d n -> p n d"),
                 in_=pos_sb[h][g][:].rearrange("p t (v d) -> p (t v) d", d=D),
             )
@@ -139,36 +137,39 @@ def tile_picked_ycblk_wts_p_kernel(
             return picked
 
         shape = [P, PACK, P]
-        pos_sum = []
-        for h in range(HALVES):
-            for g in range(2):
-                turn_positions(h, g, None)
-        for h in range(HALVES):
-            pairs = []
-            for d in (0, 2):
-                name = "pos_term%d_%d" % (h, d)
-                tile = at(4 * S * d, name, shape, F32) if h == 1 else sb(name, shape, F32)
-                term = add_position(h, d, tile, None)
-                pairs.append(add_position(h, d + 1, sb("pos_pair%d_%d" % (h, d), shape, F32), term))
-            total = sb("pos_sum%d" % h, shape, F32)
-            nc.gpsimd.tensor_tensor(out=total[:], in0=pairs[0][:], in1=pairs[1][:], op=ALU.add)
-            pos_sum.append(total)
-        scale_picked = at(8 * S + HALF, "scale_picked", [P, S], U8)
+        scale_picked = sb("scale_picked", [P, S], U8)
         nc.vector.tensor_copy(out=scale_picked[:], in_=scale_window[:].indirect(offsets[:]))
-        x_scale = sb("x_scale", [P, S], U8)
+        scale_dealt = sb("scale_dealt", [P, S], U8)
         nc.vector.tensor_copy(
-            out=x_scale[:].rearrange("p (h d v) -> p h d v", h=HALVES, d=D),
+            out=scale_dealt[:].rearrange("p (h d v) -> p h d v", h=HALVES, d=D),
             in_=scale_picked[:].rearrange("p (h v d) -> p h d v", h=HALVES, d=D),
         )
+        for o in range(PASSES):
+            for quad in range(4):
+                source, target = 16 * o + 4 * quad, 32 * quad + 4 * o
+                nc.gpsimd.dma_start(
+                    out=x_scale[target : target + 4, :].bitcast(I32),
+                    in_=scale_dealt[source : source + 4, :].bitcast(I32),
+                )
+        for h in range(HALVES):
+            for g in range(2):
+                turn_positions(h, g, "scale_window" if (h, g) == (0, 1) else None)
+        pos_sum = [None] * HALVES
+        for d in range(D):
+            for h in range(HALVES):
+                name = "pos_sum%d_%d" % (h, d)
+                place = {(1, 0): 0, (1, 2): 8 * S + 2 * HALF}
+                tile = at(place[h, d], name, shape, F32) if (h, d) in place else sb(name, shape, F32)
+                pos_sum[h] = add_position(h, d, tile, pos_sum[h])
 
         w_scale = [sb("w_scale%d" % o, [P, H], U8) for o in range(PASSES)]
         grouped = at(0, "w_grouped0", [P, H * PACK], BF16)
         cast_weights(grouped, w_first)
-        w_codes = [at(8 * S, "w_codes0", [P, H], U32)]
-        nc.vector.quantize_mx(out=w_codes[0][:].bitcast(FP8X4), scales=w_scale[0][:], in_=grouped[:])
         picked = [
-            [gather_words(0, h, at(4 * HALF * h, "x_picked0_%d" % h, [P, HALF], U32)) for h in range(HALVES)]
+            [gather_words(0, h, at(8 * S + 4 * HALF * h, "x_picked0_%d" % h, [P, HALF], U32)) for h in range(HALVES)]
         ]
+        w_codes = [at(4 * T, "w_codes0", [P, H], U32)]
+        nc.vector.quantize_mx(out=w_codes[0][:].bitcast(FP8X4), scales=w_scale[0][:], in_=grouped[:])
 
         def product(o, h, d, cols, start, stop):
             first = h * HALF + d * P
@@ -188,7 +189,7 @@ def tile_picked_ycblk_wts_p_kernel(
                 product(0, h, d, slice(0, H), True, False)
 
         picked.append(
-            [gather_words(1, h, at(4 * T + 4 * HALF * h, "x_picked1_%d" % h, [P, HALF], U32)) for h in range(HALVES)]
+            [gather_words(1, h, at(4 * HALF * h, "x_picked1_%d" % h, [P, HALF], U32)) for h in range(HALVES)]
         )
         tiles = [(h, d) for h in range(HALVES) for d in range(D)]
         w_codes.append(sb("w_codes1", [P, H], U32, tag="x_window1"))
@@ -264,10 +265,7 @@ def tile_picked_ycblk_wts_p_kernel(
             inverse = sb("inverse%d" % n, [P, 1], F32)
             nc.vector.reciprocal(out=inverse[:], in_=total[:])
             weights = sb("weights%d" % n, [P, V], F32)
-            if n == QTILES - 2:
-                nc.scalar.activation(out=weights[:], in_=ex[:], func=ACT.Copy, scale=inverse[:])
-            else:
-                nc.vector.tensor_scalar(
-                    out=weights[:], in0=ex[:], scalar1=inverse[:], scalar2=None, op0=ALU.mult
-                )
+            nc.vector.tensor_scalar(
+                out=weights[:], in0=ex[:], scalar1=inverse[:], scalar2=None, op0=ALU.mult
+            )
             nc.sync.dma_start(out=out[n * P : (n + 1) * P, :], in_=weights[:])

@@ -188,9 +188,9 @@ def tile_picked_ycblk_wts_p_kernel(
             for d in range(D):
                 product(0, h, d, slice(0, H), True, False)
 
-        picked.append(
-            [gather_words(1, h, at(4 * HALF * h, "x_picked1_%d" % h, [P, HALF], U32)) for h in range(HALVES)]
-        )
+        listed = at(0, "x_listed", [P, S], U32)
+        nc.vector.tensor_copy(out=listed[:], in_=x_window[1][:].indirect(offsets[:]))
+        picked.append([sb("x_picked1_%d" % h, [P, HALF], U32) for h in range(HALVES)])
         tiles = [(h, d) for h in range(HALVES) for d in range(D)]
         w_codes.append(sb("w_codes1", [P, H], U32, tag="x_window1"))
         for n in range(2):
@@ -198,6 +198,12 @@ def tile_picked_ycblk_wts_p_kernel(
             cast_weights(grouped, w_last[n])
             cols = slice(n * SHARE, (n + 1) * SHARE)
             nc.vector.quantize_mx(out=w_codes[1][:, cols].bitcast(FP8X4), scales=w_scale[1][:, cols], in_=grouped[:])
+            if n == 0:
+                for h in range(HALVES):
+                    nc.vector.tensor_copy(
+                        out=picked[1][h][:].bitcast(I32).rearrange("p (d v) -> p v d", d=D),
+                        in_=listed[:, h * HALF : (h + 1) * HALF].bitcast(I32).rearrange("p (v d) -> p v d", d=D),
+                    )
             for h, d in tiles[:6]:
                 product(1, h, d, cols, False, n == 1)
         for h, d in tiles[6:]:

@@ -26,6 +26,7 @@ HALVES = V // P
 HALF = S // HALVES
 QTILES = R // P
 SHARE = H // 2
+QC = R // 2
 
 
 def tile_picked_ycblk_wts_p_kernel(
@@ -68,7 +69,7 @@ def tile_picked_ycblk_wts_p_kernel(
         w_first = sb("w_first", [P, PACK, H], F32)
         w_last = [sb("w_last%d" % n, [P, PACK, SHARE], F32) for n in range(2)]
         x_window = [at(4 * T, "x_window0", [P, T], U32), sb("x_window1", [P, T], U32)]
-        q_raw = sb("q_raw", [P, PACK, R], F32)
+        q_raw = [sb("q_raw%d" % g, [P, PACK, QC], F32) for g in range(2)]
 
         def load_pos(h, g):
             nc.sync.dma_start(out=pos_sb[h][g][:], in_=pos_view[:, 2 * g : 2 * g + 2, h * HALF : (h + 1) * HALF])
@@ -93,7 +94,9 @@ def tile_picked_ycblk_wts_p_kernel(
             nc.sync.dma_start(out=x_window[o][:].bitcast(I32), in_=words)
         for n in range(2):
             load_weights(w_last[n], 1, n * SHARE, (n + 1) * SHARE)
-        nc.sync.dma_start(out=q_raw[:], in_=qT.rearrange("(p j) c -> p j c", j=PACK))
+        for g in range(2):
+            cols = qT[:, g * QC : (g + 1) * QC]
+            nc.sync.dma_start(out=q_raw[g][:], in_=cols.rearrange("(p j) c -> p j c", j=PACK))
 
         turned = [[bank(D * h + d, [P, H]) for d in range(D)] for h in range(HALVES)]
 
@@ -210,11 +213,12 @@ def tile_picked_ycblk_wts_p_kernel(
             product(1, h, d, slice(0, H), False, True)
 
         q_grouped = sb("q_grouped", [P, R * PACK], BF16, tag="w_last0")
-        nc.gpsimd.tensor_scalar(
-            out=q_grouped[:].rearrange("p (c j) -> p c j", j=PACK),
-            in0=q_raw[:].rearrange("p j c -> p c j"),
-            scalar1=1.0, scalar2=0.0, op0=ALU.mult, op1=ALU.add,
-        )
+        for g in range(2):
+            nc.gpsimd.tensor_scalar(
+                out=q_grouped[:, g * QC * PACK : (g + 1) * QC * PACK].rearrange("p (c j) -> p c j", j=PACK),
+                in0=q_raw[g][:].rearrange("p j c -> p c j"),
+                scalar1=1.0, scalar2=0.0, op0=ALU.mult, op1=ALU.add,
+            )
 
         parts = []
         for h in range(HALVES):

@@ -52,8 +52,9 @@ def tile_picked_ycblk_wts_p_kernel(
         scale_window = sb("scale_window", [P, T], U8)
         for first, last in ((32, 64), (64, P)):
             nc.vector.memset(scale_window[first:last, :].bitcast(I32), 0)
-        x_scale = sb("x_scale", [P, S], U8)
-        nc.vector.memset(x_scale[:].bitcast(I32), 0)
+        x_scale = [sb("x_scale%d" % h, [P, HALF], U8) for h in range(HALVES)]
+        for h in range(HALVES):
+            nc.vector.memset(x_scale[h][:].bitcast(I32), 0)
         warm_in = sb("warm_in", [P, 1], F32)
         warm_out = sb("warm_out", [P, 1], F32)
         nc.gpsimd.memset(warm_in[:], 0.0)
@@ -67,9 +68,7 @@ def tile_picked_ycblk_wts_p_kernel(
         pos_sb = [[sb("pos%d_%d" % (h, g), [P, 2, HALF], F32) for g in range(2)] for h in range(HALVES)]
         mix = sb("mix", [P, HALVES, D], F32)
         w_first = sb("w_first", [P, PACK, H], F32)
-        w_last = [sb("w_last%d" % n, [P, PACK, SHARE], F32) for n in range(2)]
-        x_window = [at(4 * T, "x_window0", [P, T], U32), sb("x_window1", [P, T], U32)]
-        q_raw = [sb("q_raw%d" % g, [P, PACK, QC], F32) for g in range(2)]
+        x_window = [at(4 * T, "x_window0", [P, T], U32)]
 
         def load_pos(h, g):
             nc.sync.dma_start(out=pos_sb[h][g][:], in_=pos_view[:, 2 * g : 2 * g + 2, h * HALF : (h + 1) * HALF])
@@ -78,10 +77,11 @@ def tile_picked_ycblk_wts_p_kernel(
             rows = w1[o * K_PASS : (o + 1) * K_PASS, first:last]
             nc.sync.dma_start(out=tile[:], in_=rows.rearrange("(p j) c -> p j c", j=PACK))
 
-        nc.sync.dma_start(
-            out=scale_window[0:32, :].bitcast(I32),
-            in_=x_scales.rearrange("o q n -> (o q) n").bitcast(I32),
-        )
+        for quad in range(4):
+            nc.sync.dma_start(
+                out=scale_window[8 * quad : 8 * quad + 8, :].bitcast(I32),
+                in_=x_scales[:, 4 * quad : 4 * quad + 4, :].bitcast(I32),
+            )
         nc.sync.dma_start(offsets[:], offs)
         load_pos(0, 0)
         load_pos(0, 1)
@@ -89,14 +89,12 @@ def tile_picked_ycblk_wts_p_kernel(
         load_pos(1, 0)
         load_pos(1, 1)
         load_weights(w_first, 0, 0, H)
-        for o in range(PASSES):
+
+        def load_words(o):
             words = x_words[o].rearrange("p n t -> p (n t)").bitcast(I32)
             nc.sync.dma_start(out=x_window[o][:].bitcast(I32), in_=words)
-        for n in range(2):
-            load_weights(w_last[n], 1, n * SHARE, (n + 1) * SHARE)
-        for g in range(2):
-            cols = qT[:, g * QC : (g + 1) * QC]
-            nc.sync.dma_start(out=q_raw[g][:], in_=cols.rearrange("(p j) c -> p j c", j=PACK))
+
+        load_words(0)
 
         turned = [[bank(D * h + d, [P, H]) for d in range(D)] for h in range(HALVES)]
 
@@ -140,23 +138,36 @@ def tile_picked_ycblk_wts_p_kernel(
             return picked
 
         shape = [P, PACK, P]
-        scale_picked = sb("scale_picked", [P, S], U8)
+        scale_picked = sb("scale_picked", [P, S], U8, tag="x_window1")
         nc.vector.tensor_copy(out=scale_picked[:], in_=scale_window[:].indirect(offsets[:]))
         scale_dealt = sb("scale_dealt", [P, S], U8)
         nc.vector.tensor_copy(
             out=scale_dealt[:].rearrange("p (h d v) -> p h d v", h=HALVES, d=D),
             in_=scale_picked[:].rearrange("p (h v d) -> p h d v", h=HALVES, d=D),
         )
-        for o in range(PASSES):
+
+        def move_scales(h):
             for quad in range(4):
-                source, target = 16 * o + 4 * quad, 32 * quad + 4 * o
-                nc.gpsimd.dma_start(
-                    out=x_scale[target : target + 4, :].bitcast(I32),
-                    in_=scale_dealt[source : source + 4, :].bitcast(I32),
+                nc.sync.dma_start(
+                    out=x_scale[h][32 * quad : 32 * quad + 8, :].bitcast(I32),
+                    in_=scale_dealt[8 * quad : 8 * quad + 8, h * HALF : (h + 1) * HALF].bitcast(I32),
                 )
+
         for h in range(HALVES):
             for g in range(2):
                 turn_positions(h, g, "scale_window" if (h, g) == (0, 1) else None)
+
+        move_scales(0)
+        x_window.append(sb("x_window1", [P, T], U32))
+        load_words(1)
+        move_scales(1)
+        w_last = [sb("w_last%d" % n, [P, PACK, SHARE], F32, tag="pos%d_1" % n) for n in range(2)]
+        for n in range(2):
+            load_weights(w_last[n], 1, n * SHARE, (n + 1) * SHARE)
+        q_raw = [sb("q_raw%d" % g, [P, PACK, QC], F32, tag="pos_dealt1_%d" % g) for g in range(2)]
+        for g in range(2):
+            cols = qT[:, g * QC : (g + 1) * QC]
+            nc.sync.dma_start(out=q_raw[g][:], in_=cols.rearrange("(p j) c -> p j c", j=PACK))
         pos_sum = [None] * HALVES
         for d in range(D):
             for h in range(HALVES):
@@ -175,11 +186,10 @@ def tile_picked_ycblk_wts_p_kernel(
         nc.vector.quantize_mx(out=w_codes[0][:].bitcast(FP8X4), scales=w_scale[0][:], in_=grouped[:])
 
         def product(o, h, d, cols, start, stop):
-            first = h * HALF + d * P
             nc.tensor.matmul_mx(
                 out=proj[h][d][:, cols],
                 lhsT=picked[o][h][:, d * P : (d + 1) * P].bitcast(FP8X4),
-                lhsT_scale=x_scale[4 * o : P, first : first + P],
+                lhsT_scale=x_scale[h][4 * o : P, d * P : (d + 1) * P],
                 rhs=w_codes[o][:, cols].bitcast(FP8X4),
                 rhs_scale=w_scale[o][:, cols],
                 start=start,
@@ -192,27 +202,40 @@ def tile_picked_ycblk_wts_p_kernel(
                 product(0, h, d, slice(0, H), True, False)
 
         listed = at(0, "x_listed", [P, S], U32)
-        nc.vector.tensor_copy(out=listed[:], in_=x_window[1][:].indirect(offsets[:]))
         picked.append([sb("x_picked1_%d" % h, [P, HALF], U32) for h in range(HALVES)])
-        tiles = [(h, d) for h in range(HALVES) for d in range(D)]
         w_codes.append(sb("w_codes1", [P, H], U32, tag="x_window1"))
-        for n in range(2):
-            grouped = sb("w_grouped1_%d" % n, [P, SHARE * PACK], BF16, tag=["w_first", "w_last0"][n])
+
+        def gather_plain(h):
+            cols = slice(h * HALF // 16, (h + 1) * HALF // 16)
+            nc.vector.tensor_copy(out=listed[:, h * HALF : (h + 1) * HALF], in_=x_window[1][:].indirect(offsets[:, cols]))
+
+        def deal_words(h):
+            nc.vector.tensor_copy(
+                out=picked[1][h][:].bitcast(I32).rearrange("p (d v) -> p v d", d=D),
+                in_=listed[:, h * HALF : (h + 1) * HALF].bitcast(I32).rearrange("p (v d) -> p v d", d=D),
+            )
+
+        def quantise_share(n):
+            grouped = sb("w_grouped1_%d" % n, [P, SHARE * PACK], BF16, tag=["w_first", "pos0_1"][n])
             cast_weights(grouped, w_last[n])
             cols = slice(n * SHARE, (n + 1) * SHARE)
             nc.vector.quantize_mx(out=w_codes[1][:, cols].bitcast(FP8X4), scales=w_scale[1][:, cols], in_=grouped[:])
-            if n == 0:
-                for h in range(HALVES):
-                    nc.vector.tensor_copy(
-                        out=picked[1][h][:].bitcast(I32).rearrange("p (d v) -> p v d", d=D),
-                        in_=listed[:, h * HALF : (h + 1) * HALF].bitcast(I32).rearrange("p (v d) -> p v d", d=D),
-                    )
-            for h, d in tiles[:6]:
-                product(1, h, d, cols, False, n == 1)
-        for h, d in tiles[6:]:
-            product(1, h, d, slice(0, H), False, True)
+            return cols
 
-        q_grouped = sb("q_grouped", [P, R * PACK], BF16, tag="w_last0")
+        gather_plain(0)
+        deal_words(0)
+        gather_plain(1)
+        cols = quantise_share(0)
+        for d in range(D):
+            product(1, 0, d, cols, False, False)
+        deal_words(1)
+        cols = quantise_share(1)
+        for d in range(D):
+            product(1, 0, d, cols, False, True)
+        for d in range(D):
+            product(1, 1, d, slice(0, H), False, True)
+
+        q_grouped = sb("q_grouped", [P, R * PACK], BF16, tag="pos0_1")
         for g in range(2):
             nc.gpsimd.tensor_scalar(
                 out=q_grouped[:, g * QC * PACK : (g + 1) * QC * PACK].rearrange("p (c j) -> p c j", j=PACK),

@@ -27,6 +27,7 @@ HALF = S // HALVES
 QTILES = R // P
 SHARE = H // 2
 QC = R // 2
+SCALAR_COLS = 160
 
 
 def tile_picked_ycblk_wts_p_kernel(
@@ -52,9 +53,8 @@ def tile_picked_ycblk_wts_p_kernel(
         scale_window = sb("scale_window", [P, T], U8)
         for first, last in ((32, 64), (64, P)):
             nc.vector.memset(scale_window[first:last, :].bitcast(I32), 0)
-        x_scale = [sb("x_scale%d" % h, [P, HALF], U8) for h in range(HALVES)]
-        for h in range(HALVES):
-            nc.vector.memset(x_scale[h][:].bitcast(I32), 0)
+        x_scale = sb("x_scale", [P, S], U8)
+        nc.vector.memset(x_scale[:].bitcast(I32), 0)
         warm_in = sb("warm_in", [P, 1], F32)
         warm_out = sb("warm_out", [P, 1], F32)
         nc.gpsimd.memset(warm_in[:], 0.0)
@@ -65,29 +65,26 @@ def tile_picked_ycblk_wts_p_kernel(
 
 
         pos_view = pos.rearrange("(p t) j -> p t j", t=PACK)
-        pos_sb = [[sb("pos%d_%d" % (h, g), [P, 2, HALF], F32) for g in range(2)] for h in range(HALVES)]
+        pos_sb = [sb("pos%d" % g, [P, 2, S], F32) for g in range(2)]
         mix = sb("mix", [P, HALVES, D], F32)
         w_first = sb("w_first", [P, PACK, H], F32)
         x_window = [at(4 * T, "x_window0", [P, T], U32)]
 
-        def load_pos(h, g):
-            nc.sync.dma_start(out=pos_sb[h][g][:], in_=pos_view[:, 2 * g : 2 * g + 2, h * HALF : (h + 1) * HALF])
+        def load_pos(g):
+            nc.sync.dma_start(out=pos_sb[g][:], in_=pos_view[:, 2 * g : 2 * g + 2, :])
 
         def load_weights(tile, o, first, last):
             rows = w1[o * K_PASS : (o + 1) * K_PASS, first:last]
             nc.sync.dma_start(out=tile[:], in_=rows.rearrange("(p j) c -> p j c", j=PACK))
 
-        for quad in range(4):
-            nc.sync.dma_start(
-                out=scale_window[8 * quad : 8 * quad + 8, :].bitcast(I32),
-                in_=x_scales[:, 4 * quad : 4 * quad + 4, :].bitcast(I32),
-            )
+        nc.sync.dma_start(
+            out=scale_window[0:32, :].bitcast(I32),
+            in_=x_scales.rearrange("o q n -> (o q) n").bitcast(I32),
+        )
         nc.sync.dma_start(offsets[:], offs)
-        load_pos(0, 0)
-        load_pos(0, 1)
+        load_pos(0)
         nc.sync.dma_start(out=mix[:], in_=mixw[0, :].rearrange("(h v d) -> v h d", h=HALVES, d=D))
-        load_pos(1, 0)
-        load_pos(1, 1)
+        load_pos(1)
         load_weights(w_first, 0, 0, H)
 
         def load_words(o):
@@ -95,15 +92,25 @@ def tile_picked_ycblk_wts_p_kernel(
             nc.sync.dma_start(out=x_window[o][:].bitcast(I32), in_=words)
 
         load_words(0)
+        x_window.append(sb("x_window1", [P, T], U32))
+        load_words(1)
+        w_last = []
+        for n in range(2):
+            w_last.append(sb("w_last%d" % n, [P, PACK, SHARE], F32))
+            load_weights(w_last[n], 1, n * SHARE, (n + 1) * SHARE)
+        q_raw = []
+        for g in range(2):
+            q_raw.append(sb("q_raw%d" % g, [P, PACK, QC], F32))
+            cols = qT[:, g * QC : (g + 1) * QC]
+            nc.sync.dma_start(out=q_raw[g][:], in_=cols.rearrange("(p j) c -> p j c", j=PACK))
 
         turned = [[bank(D * h + d, [P, H]) for d in range(D)] for h in range(HALVES)]
 
-        def turn_positions(h, g, tag):
-            dealt = sb("pos_dealt%d_%d" % (h, g), [P, D, 2 * P], F32, tag=tag)
-            copy = nc.scalar.copy if g == 0 else nc.vector.tensor_copy
-            copy(
-                out=dealt[:].rearrange("p d n -> p n d"),
-                in_=pos_sb[h][g][:].rearrange("p t (v d) -> p (t v) d", d=D),
+        def turn_positions(h, g):
+            dealt = sb("pos_dealt%d_%d" % (h, g), [P, D, 2 * P], F32)
+            nc.scalar.copy(
+                out=dealt[:].rearrange("p d (t v) -> p t v d", t=2),
+                in_=pos_sb[g][:, :, h * HALF : (h + 1) * HALF].rearrange("p t (v d) -> p t v d", d=D),
             )
             for d in range(D):
                 for t in range(2):
@@ -123,73 +130,71 @@ def tile_picked_ycblk_wts_p_kernel(
         def add_position(h, d, total, prior):
             return weigh(total, turned[h][d][:].rearrange("v (t p) -> v t p", t=PACK), h, d, prior)
 
-        def cast_weights(grouped, raw):
-            nc.scalar.copy(
-                out=grouped[:].rearrange("p (c i j) -> p c j i", i=4, j=PACK),
-                in_=raw[:].rearrange("p j (c i) -> p c j i", i=4),
+        def cast_weights(copy, grouped, raw, first, last):
+            copy(
+                out=grouped[:, first * PACK : last * PACK].rearrange("p (c i j) -> p c j i", i=4, j=PACK),
+                in_=raw[:, :, first:last].rearrange("p j (c i) -> p c j i", i=4),
             )
 
-        def gather_words(o, h, picked):
+        def gather_words(o, h, listed):
             cols = slice(h * HALF // 16, (h + 1) * HALF // 16)
+            nc.vector.tensor_copy(out=listed, in_=x_window[o][:].indirect(offsets[:, cols]))
+
+        def deal_words(picked, listed):
             nc.vector.tensor_copy(
-                out=picked[:].rearrange("p (d v) -> p v d", d=D),
-                in_=x_window[o][:].indirect(offsets[:, cols]),
+                out=picked[:].bitcast(I32).rearrange("p (d v) -> p v d", d=D),
+                in_=listed.bitcast(I32).rearrange("p (v d) -> p v d", d=D),
             )
-            return picked
 
         shape = [P, PACK, P]
-        scale_picked = sb("scale_picked", [P, S], U8, tag="x_window1")
+        scale_picked = sb("scale_picked", [P, S], U8)
         nc.vector.tensor_copy(out=scale_picked[:], in_=scale_window[:].indirect(offsets[:]))
         scale_dealt = sb("scale_dealt", [P, S], U8)
         nc.vector.tensor_copy(
             out=scale_dealt[:].rearrange("p (h d v) -> p h d v", h=HALVES, d=D),
             in_=scale_picked[:].rearrange("p (h v d) -> p h d v", h=HALVES, d=D),
         )
-
-        def move_scales(h):
+        for o in range(PASSES):
             for quad in range(4):
-                nc.sync.dma_start(
-                    out=x_scale[h][32 * quad : 32 * quad + 8, :].bitcast(I32),
-                    in_=scale_dealt[8 * quad : 8 * quad + 8, h * HALF : (h + 1) * HALF].bitcast(I32),
+                source, target = 16 * o + 4 * quad, 32 * quad + 4 * o
+                nc.gpsimd.dma_start(
+                    out=x_scale[target : target + 4, :].bitcast(I32),
+                    in_=scale_dealt[source : source + 4, :].bitcast(I32),
                 )
-
-        for h in range(HALVES):
-            for g in range(2):
-                turn_positions(h, g, "scale_window" if (h, g) == (0, 1) else None)
-
-        move_scales(0)
-        x_window.append(sb("x_window1", [P, T], U32))
-        load_words(1)
-        move_scales(1)
-        w_last = [sb("w_last%d" % n, [P, PACK, SHARE], F32, tag="pos%d_1" % n) for n in range(2)]
-        for n in range(2):
-            load_weights(w_last[n], 1, n * SHARE, (n + 1) * SHARE)
-        q_raw = [sb("q_raw%d" % g, [P, PACK, QC], F32, tag="pos_dealt1_%d" % g) for g in range(2)]
         for g in range(2):
-            cols = qT[:, g * QC : (g + 1) * QC]
-            nc.sync.dma_start(out=q_raw[g][:], in_=cols.rearrange("(p j) c -> p j c", j=PACK))
-        pos_sum = [None] * HALVES
-        for d in range(D):
             for h in range(HALVES):
-                name = "pos_sum%d_%d" % (h, d)
-                place = {(1, 0): 0, (1, 2): 8 * S + 2 * HALF}
-                tile = at(place[h, d], name, shape, F32) if (h, d) in place else sb(name, shape, F32)
-                pos_sum[h] = add_position(h, d, tile, pos_sum[h])
+                turn_positions(h, g)
+        pos_sum = [None] * HALVES
+        place = {(1, 0): 0, (1, 1): 8 * S, (0, 2): 8 * S + 4 * HALF, (1, 3): 5 * T}
+
+        def position_term(h, d):
+            name = "pos_sum%d_%d" % (h, d)
+            tile = at(place[h, d], name, shape, F32) if (h, d) in place else sb(name, shape, F32)
+            pos_sum[h] = add_position(h, d, tile, pos_sum[h])
+
+        terms = [(h, d) for d in range(D) for h in range(HALVES)]
+        for h, d in terms[:-1]:
+            position_term(h, d)
 
         w_scale = [sb("w_scale%d" % o, [P, H], U8) for o in range(PASSES)]
         grouped = at(0, "w_grouped0", [P, H * PACK], BF16)
-        cast_weights(grouped, w_first)
-        picked = [
-            [gather_words(0, h, at(8 * S + 4 * HALF * h, "x_picked0_%d" % h, [P, HALF], U32)) for h in range(HALVES)]
-        ]
+        cast_weights(nc.scalar.copy, grouped, w_first, 0, H)
+        picked = [[sb("x_picked0_%d" % h, [P, HALF], U32) for h in range(HALVES)], [sb("x_picked1_0", [P, HALF], U32)]]
+        first_listed = [at(8 * S + 4 * HALF * h, "x_listed0_%d" % h, [P, HALF], U32) for h in range(HALVES)]
+        for h in range(HALVES):
+            gather_words(0, h, first_listed[h][:])
+        for h in range(HALVES):
+            deal_words(picked[0][h], first_listed[h][:])
+        position_term(*terms[-1])
         w_codes = [at(4 * T, "w_codes0", [P, H], U32)]
         nc.vector.quantize_mx(out=w_codes[0][:].bitcast(FP8X4), scales=w_scale[0][:], in_=grouped[:])
 
         def product(o, h, d, cols, start, stop):
+            first = h * HALF + d * P
             nc.tensor.matmul_mx(
                 out=proj[h][d][:, cols],
                 lhsT=picked[o][h][:, d * P : (d + 1) * P].bitcast(FP8X4),
-                lhsT_scale=x_scale[h][4 * o : P, d * P : (d + 1) * P],
+                lhsT_scale=x_scale[4 * o : P, first : first + P],
                 rhs=w_codes[o][:, cols].bitcast(FP8X4),
                 rhs_scale=w_scale[o][:, cols],
                 start=start,
@@ -202,40 +207,37 @@ def tile_picked_ycblk_wts_p_kernel(
                 product(0, h, d, slice(0, H), True, False)
 
         listed = at(0, "x_listed", [P, S], U32)
-        picked.append([sb("x_picked1_%d" % h, [P, HALF], U32) for h in range(HALVES)])
         w_codes.append(sb("w_codes1", [P, H], U32, tag="x_window1"))
+        halves = [listed[:, h * HALF : (h + 1) * HALF] for h in range(HALVES)]
 
-        def gather_plain(h):
-            cols = slice(h * HALF // 16, (h + 1) * HALF // 16)
-            nc.vector.tensor_copy(out=listed[:, h * HALF : (h + 1) * HALF], in_=x_window[1][:].indirect(offsets[:, cols]))
-
-        def deal_words(h):
-            nc.vector.tensor_copy(
-                out=picked[1][h][:].bitcast(I32).rearrange("p (d v) -> p v d", d=D),
-                in_=listed[:, h * HALF : (h + 1) * HALF].bitcast(I32).rearrange("p (v d) -> p v d", d=D),
-            )
+        shares = [slice(n * SHARE, (n + 1) * SHARE) for n in range(2)]
+        last_grouped = []
+        for n in range(2):
+            last_grouped.append(sb("w_grouped1_%d" % n, [P, SHARE * PACK], BF16, tag=["w_first", "w_grouped1_1"][n]))
+            cast_weights(nc.scalar.copy, last_grouped[n], w_last[n], 0, [SHARE, SCALAR_COLS][n])
 
         def quantise_share(n):
-            grouped = sb("w_grouped1_%d" % n, [P, SHARE * PACK], BF16, tag=["w_first", "pos0_1"][n])
-            cast_weights(grouped, w_last[n])
-            cols = slice(n * SHARE, (n + 1) * SHARE)
-            nc.vector.quantize_mx(out=w_codes[1][:, cols].bitcast(FP8X4), scales=w_scale[1][:, cols], in_=grouped[:])
-            return cols
+            cols = shares[n]
+            nc.vector.quantize_mx(
+                out=w_codes[1][:, cols].bitcast(FP8X4), scales=w_scale[1][:, cols], in_=last_grouped[n][:]
+            )
 
-        gather_plain(0)
-        deal_words(0)
-        gather_plain(1)
-        cols = quantise_share(0)
+        for h in range(HALVES):
+            gather_words(1, h, halves[h])
+        deal_words(picked[1][0], halves[0])
+        quantise_share(0)
         for d in range(D):
-            product(1, 0, d, cols, False, False)
-        deal_words(1)
-        cols = quantise_share(1)
+            product(1, 0, d, shares[0], False, False)
+        cast_weights(nc.vector.tensor_copy, last_grouped[1], w_last[1], SCALAR_COLS, SHARE)
+        quantise_share(1)
         for d in range(D):
-            product(1, 0, d, cols, False, True)
+            product(1, 0, d, shares[1], False, True)
+        picked[1].append(sb("x_picked1_1", [P, HALF], U32, tag="w_grouped1_1"))
+        deal_words(picked[1][1], halves[1])
         for d in range(D):
             product(1, 1, d, slice(0, H), False, True)
 
-        q_grouped = sb("q_grouped", [P, R * PACK], BF16, tag="pos0_1")
+        q_grouped = at(0, "q_grouped", [P, R * PACK], BF16)
         for g in range(2):
             nc.gpsimd.tensor_scalar(
                 out=q_grouped[:, g * QC * PACK : (g + 1) * QC * PACK].rearrange("p (c j) -> p c j", j=PACK),

@@ -27,6 +27,7 @@ HALF = S // HALVES
 QTILES = R // P
 SHARE = H // 2
 QC = R // 2
+EARLY_TILES = 2
 SCALAR_COLS = 160
 
 
@@ -277,26 +278,48 @@ def tile_picked_ycblk_wts_p_kernel(
             k_codes.append(codes)
             k_scale.append(scale)
 
-        scores = [bank(n, [P, V]) for n in (2, 3, 6, 7)]
-        for h in range(HALVES):
-            for n in range(QTILES):
-                nc.tensor.matmul_mx(
-                    out=scores[n][:, h * P : (h + 1) * P],
-                    lhsT=q_codes[:, n * P : (n + 1) * P].bitcast(FP8X4),
-                    lhsT_scale=q_scale[:, n * P : (n + 1) * P],
-                    rhs=k_codes[h][:].bitcast(FP8X4),
-                    rhs_scale=k_scale[h][:],
-                    start=True,
-                    stop=True,
-                )
+        def score(target, n, h):
+            nc.tensor.matmul_mx(
+                out=target,
+                lhsT=q_codes[:, n * P : (n + 1) * P].bitcast(FP8X4),
+                lhsT_scale=q_scale[:, n * P : (n + 1) * P],
+                rhs=k_codes[h][:].bitcast(FP8X4),
+                rhs_scale=k_scale[h][:],
+                start=True,
+                stop=True,
+            )
+
+        def negate(negated, least, source, h, prior):
+            nc.vector.tensor_scalar(
+                out=negated[:, h * P : (h + 1) * P], in0=source, scalar1=-1.0, scalar2=prior,
+                op0=ALU.mult, op1=ALU.min, accum_out=least[:],
+            )
+
+        early = bank(2, [P, EARLY_TILES, P])
+        scores = [bank(3 + n, [P, P] if n < EARLY_TILES else [P, V]) for n in range(QTILES)]
         for n in range(QTILES):
-            neg_max = sb("neg_max%d" % n, [P, 1], F32)
-            nc.vector.tensor_reduce(out=neg_max[:], in_=scores[n][:], axis=AX.X, op=ALU.max, negate=True)
+            score(early[:, n, :] if n < EARLY_TILES else scores[n][:, 0:P], n, 0)
+        for n in range(QTILES):
+            score(scores[n][:] if n < EARLY_TILES else scores[n][:, P:V], n, 1)
+        negated, first_least = [], []
+        for n in range(EARLY_TILES):
+            negated.append(sb("negated%d" % n, [P, V], F32, tag="k_grouped1" if n == 0 else None))
+            first_least.append(sb("first_least%d" % n, [P, 1], F32))
+            negate(negated[n], first_least[n], early[:, n, :], 0, None)
+        for n in range(QTILES):
+            shift = sb("shift%d" % n, [P, 1], F32)
             ex = sb("ex%d" % n, [P, V], F32)
             total = sb("total%d" % n, [P, 1], F32)
-            nc.scalar.activation(
-                out=ex[:], in_=scores[n][:], func=ACT.Exp, bias=neg_max[:], accum_out=total[:]
-            )
+            if n < EARLY_TILES:
+                negate(negated[n], shift, scores[n][:], 1, first_least[n][:])
+                nc.scalar.activation(
+                    out=ex[:], in_=negated[n][:], func=ACT.Exp, scale=-1.0, bias=shift[:], accum_out=total[:]
+                )
+            else:
+                nc.vector.tensor_reduce(out=shift[:], in_=scores[n][:], axis=AX.X, op=ALU.max, negate=True)
+                nc.scalar.activation(
+                    out=ex[:], in_=scores[n][:], func=ACT.Exp, bias=shift[:], accum_out=total[:]
+                )
             inverse = sb("inverse%d" % n, [P, 1], F32)
             nc.vector.reciprocal(out=inverse[:], in_=total[:])
             weights = sb("weights%d" % n, [P, V], F32)

@@ -67,7 +67,7 @@ def tile_picked_ycblk_wts_p_kernel(
 
         pos_view = pos.rearrange("(p t) j -> p t j", t=PACK)
         pos_sb = [sb("pos%d" % g, [P, 2, S], F32) for g in range(2)]
-        mix = sb("mix", [P, HALVES, D], F32)
+        mix = sb("mix", [P, HALVES, 2 * D], F32)
         w_first = sb("w_first", [P, PACK, H], F32)
         x_window = [at(4 * T, "x_window0", [P, T], U32)]
 
@@ -84,7 +84,7 @@ def tile_picked_ycblk_wts_p_kernel(
         )
         nc.sync.dma_start(offsets[:], offs)
         load_pos(0)
-        nc.sync.dma_start(out=mix[:], in_=mixw[0, :].rearrange("(h v d) -> v h d", h=HALVES, d=D))
+        nc.sync.dma_start(out=mix[:, :, 0:D], in_=mixw[0, :].rearrange("(h v d) -> v h d", h=HALVES, d=D))
         load_pos(1)
         load_weights(w_first, 0, 0, H)
 

@@ -29,6 +29,7 @@ SHARE = H // 2
 QC = R // 2
 EARLY_TILES = 2
 SCALAR_COLS = 160
+JOINED = 2
 
 
 def tile_picked_ycblk_wts_p_kernel(
@@ -121,15 +122,16 @@ def tile_picked_ycblk_wts_p_kernel(
         def weigh(total, source, h, d, prior):
             weight = mix[:, h, d : d + 1]
             if prior is None:
-                nc.scalar.activation(out=total[:], in_=source, func=ACT.Copy, scale=weight)
+                nc.scalar.activation(out=total, in_=source, func=ACT.Copy, scale=weight)
             else:
                 nc.vector.scalar_tensor_tensor(
-                    out=total[:], in0=source, scalar=weight, in1=prior[:], op0=ALU.mult, op1=ALU.add
+                    out=total, in0=source, scalar=weight, in1=prior, op0=ALU.mult, op1=ALU.add
                 )
-            return total
 
         def add_position(h, d, total, prior):
-            return weigh(total, turned[h][d][:].rearrange("v (t p) -> v t p", t=PACK), h, d, prior)
+            source = turned[h][d][:].rearrange("v (t p) -> v t p", t=PACK)
+            weigh(total[:], source, h, d, None if prior is None else prior[:])
+            return total
 
         def cast_weights(copy, grouped, raw, first, last):
             copy(
@@ -246,27 +248,35 @@ def tile_picked_ycblk_wts_p_kernel(
                 scalar1=1.0, scalar2=0.0, op0=ALU.mult, op1=ALU.add,
             )
 
+        every, alone, joined = slice(0, PACK), slice(0, PACK - JOINED), slice(PACK - JOINED, PACK)
+
+        def read(name, h, d, prior, planes):
+            total = sb(name, shape, F32)
+            source = proj[h][d][:].rearrange("v (p t) -> v t p", t=PACK)[:, planes, :]
+            weigh(total[:, planes, :], source, h, d, None if prior is None else prior[:, planes, :])
+            return total
+
         parts = []
         for h in range(HALVES):
-            part = {}
-            for d in range(D):
-                prior = {0: None, 1: pos_sum[h], 2: None, 3: part.get(0)}[d]
-                source = proj[h][d][:].rearrange("v (p t) -> v t p", t=PACK)
-                part[d] = weigh(sb("part%d_%d" % (h, d), shape, F32), source, h, d, prior)
-            parts.append([part[1], part[2], part[3]])
-        q_codes = sb("q_codes", [P, R], U32, tag="part1_0")
+            single = read("part%d_0" % h, h, 0, None, every)
+            first = read("part%d_1" % h, h, 1, pos_sum[h], every)
+            kept = every if h == 0 else alone
+            second = read("part%d_2" % h, h, 2, None, kept)
+            third = read("part%d_3" % h, h, 3, single, every)
+            parts.append([(first, kept), (second, kept), (third, every)])
+        parts[1].append((read("part1_4", 1, 2, first, joined), joined))
+        q_codes = sb("q_codes", [P, R], U32, tag="part1_1")
         q_scale = sb("q_scale", [P, R], U8)
         nc.vector.quantize_mx(out=q_codes[:].bitcast(FP8X4), scales=q_scale[:], in_=q_grouped[:])
         k_codes, k_scale = [], []
         for h in range(HALVES):
             keys = bank(h, shape)
-            for n, part in enumerate(parts[h]):
-                for t in range(PACK):
-                    nc.tensor.matmul(
-                        out=keys[:, t, :], lhsT=part[:, t, :], rhs=ident[:], is_transpose=True,
-                        start=(n == 0 and t == 0),
-                        stop=(n == len(parts[h]) - 1 and t == PACK - 1),
-                    )
+            turns = [(part, t) for part, planes in parts[h] for t in range(planes.start, planes.stop)]
+            for n, (part, t) in enumerate(turns):
+                nc.tensor.matmul(
+                    out=keys[:, t, :], lhsT=part[:, t, :], rhs=ident[:], is_transpose=True,
+                    start=(n == 0), stop=(n == len(turns) - 1),
+                )
             grouped = sb("k_grouped%d" % h, [P, P * PACK], BF16)
             nc.scalar.copy(
                 out=grouped[:].rearrange("p (v t) -> p v t", t=PACK),

from contextlib import ExitStack

import concourse.mybir as mybir
from concourse.masks import make_identity

K, T, S, D, H, R = 1024, 4096, 1024, 4, 512, 512
V = S // D
FLOPS = 2 * K * H * S + 2 * H * R * V

F32 = mybir.dt.float32
BF16 = mybir.dt.bfloat16
I32 = mybir.dt.int32
U32 = mybir.dt.uint32
U16 = mybir.dt.uint16
U8 = mybir.dt.uint8
FP8X4 = mybir.dt.float8_e4m3fn_x4
ALU = mybir.AluOpType
ACT = mybir.ActivationFunctionType
AX = mybir.AxisListType

P = 128
PACK = 4
K_PASS = P * PACK
PASSES = K // K_PASS
HALVES = V // P
HALF = S // HALVES
QTILES = R // P
SHARE = H // 2
QC = R // 2
EARLY_TILES = 2
SCALAR_COLS = 160
JOINED = 2


def tile_picked_ycblk_wts_p_kernel(
    tc, x_words, x_scales, w1, pos, mixw, qT, offs, out
):
    nc = tc.nc
    with ExitStack() as ctx:
        keep = ctx.enter_context(tc.tile_pool(name="keep", bufs=1))
        placed = ctx.enter_context(tc.tile_pool(name="placed", bufs=1))
        psum = ctx.enter_context(tc.psum_pool(name="psum", bufs=1))

        def sb(name, shape, dtype, tag=None):
            return keep.tile(shape, dtype, name=name, tag=tag or name, align_bytes=64)

        def at(offset, name, shape, dtype):
            return placed.tile(shape, dtype, name=name, offset=offset, align_bytes=64)

        def bank(index, shape):
            return psum.tile(shape, F32, name="bank%d" % index, tag="bank%d" % index)

        offsets = keep.tile([P, S // 16], U16, name="offsets")

        scale_window = sb("scale_window", [P, T], U8)
        for first, last in ((32, 64), (64, P)):
            nc.vector.memset(scale_window[first:last, :].bitcast(I32), 0)
        x_scale = sb("x_scale", [P, S], U8)
        nc.vector.memset(x_scale[:].bitcast(I32), 0)
        warm_in = sb("warm_in", [P, 1], F32)
        warm_out = sb("warm_out", [P, 1], F32)
        nc.gpsimd.memset(warm_in[:], 0.0)
        nc.scalar.activation(out=warm_out[:], in_=warm_in[:], func=ACT.Exp)

        ident = sb("ident", [P, P], F32)
        make_identity(nc, ident[:])


        pos_view = pos.rearrange("(p t) j -> p t j", t=PACK)
        pos_sb = [sb("pos%d" % g, [P, 2, S], F32) for g in range(2)]
        mix = sb("mix", [P, HALVES, 2 * D], F32)
        w_first = sb("w_first", [P, PACK, H], F32)
        x_window = [at(4 * T, "x_window0", [P, T], U32)]

        def load_pos(g):
            nc.sync.dma_start(out=pos_sb[g][:], in_=pos_view[:, 2 * g : 2 * g + 2, :])

        def load_weights(tile, o, first, last):
            rows = w1[o * K_PASS : (o + 1) * K_PASS, first:last]
            nc.sync.dma_start(out=tile[:], in_=rows.rearrange("(p j) c -> p j c", j=PACK))

        nc.sync.dma_start(
            out=scale_window[0:32, :].bitcast(I32),
            in_=x_scales.rearrange("o q n -> (o q) n").bitcast(I32),
        )
        nc.sync.dma_start(offsets[:], offs)
        load_pos(0)
        nc.sync.dma_start(out=mix[:, :, 0:D], in_=mixw[0, :].rearrange("(h v d) -> v h d", h=HALVES, d=D))
        load_pos(1)
        load_weights(w_first, 0, 0, H)

        def load_words(o):
            words = x_words[o].rearrange("p n t -> p (n t)").bitcast(I32)
            nc.sync.dma_start(out=x_window[o][:].bitcast(I32), in_=words)

        load_words(0)
        x_window.append(sb("x_window1", [P, T], U32))
        load_words(1)
        w_last = []
        for n in range(2):
            w_last.append(sb("w_last%d" % n, [P, PACK, SHARE], F32))
            load_weights(w_last[n], 1, n * SHARE, (n + 1) * SHARE)
        q_raw = []
        for g in range(2):
            q_raw.append(sb("q_raw%d" % g, [P, PACK, QC], F32))
            cols = qT[:, g * QC : (g + 1) * QC]
            nc.sync.dma_start(out=q_raw[g][:], in_=cols.rearrange("(p j) c -> p j c", j=PACK))

        turned = [[bank(D * h + d, [P, H]) for d in range(D)] for h in range(HALVES)]

        def turn_positions(h, g):
            dealt = sb("pos_dealt%d_%d" % (h, g), [P, D, 2 * P], F32)
            nc.scalar.copy(
                out=dealt[:].rearrange("p d (t v) -> p t v d", t=2),
                in_=pos_sb[g][:, :, h * HALF : (h + 1) * HALF].rearrange("p t (v d) -> p t v d", d=D),
            )
            for d in range(D):
                for t in range(2):
                    cols = slice((2 * g + t) * P, (2 * g + t + 1) * P)
                    nc.tensor.transpose(turned[h][d][:, cols], dealt[:, d, t * P : (t + 1) * P], ident[:])

        def weigh(total, source, h, d, prior):
            weight = mix[:, h, d : d + 1]
            if prior is None:
                nc.scalar.activation(out=total, in_=source, func=ACT.Copy, scale=weight)
            else:
                nc.vector.scalar_tensor_tensor(
                    out=total, in0=source, scalar=weight, in1=prior, op0=ALU.mult, op1=ALU.add
                )

        def add_position(h, d, total, prior):
            source = turned[h][d][:].rearrange("v (t p) -> v t p", t=PACK)
            weigh(total[:], source, h, d, None if prior is None else prior[:])
            return total

        def cast_weights(copy, grouped, raw, first, last):
            copy(
                out=grouped[:, first * PACK : last * PACK].rearrange("p (c i j) -> p c j i", i=4, j=PACK),
                in_=raw[:, :, first:last].rearrange("p j (c i) -> p c j i", i=4),
            )

        def gather_words(o, h, listed):
            cols = slice(h * HALF // 16, (h + 1) * HALF // 16)
            nc.vector.tensor_copy(out=listed, in_=x_window[o][:].indirect(offsets[:, cols]))

        def deal_words(picked, listed):
            nc.vector.tensor_copy(
                out=picked[:].bitcast(I32).rearrange("p (d v) -> p v d", d=D),
                in_=listed.bitcast(I32).rearrange("p (v d) -> p v d", d=D),
            )

        shape = [P, PACK, P]
        scale_picked = sb("scale_picked", [P, S], U8)
        nc.vector.tensor_copy(out=scale_picked[:], in_=scale_window[:].indirect(offsets[:]))
        scale_dealt = sb("scale_dealt", [P, S], U8)
        nc.vector.tensor_copy(
            out=scale_dealt[:].rearrange("p (h d v) -> p h d v", h=HALVES, d=D),
            in_=scale_picked[:].rearrange("p (h v d) -> p h d v", h=HALVES, d=D),
        )
        for o in range(PASSES):
            for quad in range(4):
                source, target = 16 * o + 4 * quad, 32 * quad + 4 * o
                nc.gpsimd.dma_start(
                    out=x_scale[target : target + 4, :].bitcast(I32),
                    in_=scale_dealt[source : source + 4, :].bitcast(I32),
                )
        for g in range(2):
            for h in range(HALVES):
                turn_positions(h, g)
        pos_sum = [None] * HALVES
        place = {(1, 0): 0, (1, 1): 8 * S, (0, 2): 8 * S + 4 * HALF, (1, 3): 5 * T}

        def position_term(h, d):
            name = "pos_sum%d_%d" % (h, d)
            tile = at(place[h, d], name, shape, F32) if (h, d) in place else sb(name, shape, F32)
            pos_sum[h] = add_position(h, d, tile, pos_sum[h])

        terms = [(h, d) for d in range(D) for h in range(HALVES)]
        for h, d in terms[:-1]:
            position_term(h, d)

        w_scale = [sb("w_scale%d" % o, [P, H], U8) for o in range(PASSES)]
        grouped = at(0, "w_grouped0", [P, H * PACK], BF16)
        cast_weights(nc.scalar.copy, grouped, w_first, 0, H)
        picked = [[sb("x_picked0_%d" % h, [P, HALF], U32) for h in range(HALVES)], [sb("x_picked1_0", [P, HALF], U32)]]
        first_listed = [at(8 * S + 4 * HALF * h, "x_listed0_%d" % h, [P, HALF], U32) for h in range(HALVES)]
        for h in range(HALVES):
            gather_words(0, h, first_listed[h][:])
        for h in range(HALVES):
            deal_words(picked[0][h], first_listed[h][:])
        position_term(*terms[-1])
        w_codes = [at(4 * T, "w_codes0", [P, H], U32)]
        nc.vector.quantize_mx(out=w_codes[0][:].bitcast(FP8X4), scales=w_scale[0][:], in_=grouped[:])

        def product(o, h, d, cols, start, stop):
            first = h * HALF + d * P
            nc.tensor.matmul_mx(
                out=proj[h][d][:, cols],
                lhsT=picked[o][h][:, d * P : (d + 1) * P].bitcast(FP8X4),
                lhsT_scale=x_scale[4 * o : P, first : first + P],
                rhs=w_codes[o][:, cols].bitcast(FP8X4),
                rhs_scale=w_scale[o][:, cols],
                start=start,
                stop=stop,
            )

        proj = [[bank(D * h + d, [P, H]) for d in range(D)] for h in range(HALVES)]
        for h in range(HALVES):
            for d in range(D):
                product(0, h, d, slice(0, H), True, False)

        listed = at(0, "x_listed", [P, S], U32)
        w_codes.append(sb("w_codes1", [P, H], U32, tag="x_window1"))
        halves = [listed[:, h * HALF : (h + 1) * HALF] for h in range(HALVES)]

        shares = [slice(n * SHARE, (n + 1) * SHARE) for n in range(2)]
        last_grouped = []
        for n in range(2):
            last_grouped.append(sb("w_grouped1_%d" % n, [P, SHARE * PACK], BF16, tag=["w_first", "w_grouped1_1"][n]))
            cast_weights(nc.scalar.copy, last_grouped[n], w_last[n], 0, [SHARE, SCALAR_COLS][n])

        def quantise_share(n):
            cols = shares[n]
            nc.vector.quantize_mx(
                out=w_codes[1][:, cols].bitcast(FP8X4), scales=w_scale[1][:, cols], in_=last_grouped[n][:]
            )

        for h in range(HALVES):
            gather_words(1, h, halves[h])
        deal_words(picked[1][0], halves[0])
        quantise_share(0)
        for d in range(D):
            product(1, 0, d, shares[0], False, False)
        cast_weights(nc.vector.tensor_copy, last_grouped[1], w_last[1], SCALAR_COLS, SHARE)
        quantise_share(1)
        for d in range(D):
            product(1, 0, d, shares[1], False, True)
        picked[1].append(sb("x_picked1_1", [P, HALF], U32, tag="w_grouped1_1"))
        deal_words(picked[1][1], halves[1])
        for d in range(D):
            product(1, 1, d, slice(0, H), False, True)

        q_grouped = at(0, "q_grouped", [P, R * PACK], BF16)
        for g in range(2):
            nc.gpsimd.tensor_scalar(
                out=q_grouped[:, g * QC * PACK : (g + 1) * QC * PACK].rearrange("p (c j) -> p c j", j=PACK),
                in0=q_raw[g][:].rearrange("p j c -> p c j"),
                scalar1=1.0, scalar2=0.0, op0=ALU.mult, op1=ALU.add,
            )

        every, alone, joined = slice(0, PACK), slice(0, PACK - JOINED), slice(PACK - JOINED, PACK)

        def read(name, h, d, prior, planes):
            total = sb(name, shape, F32)
            source = proj[h][d][:].rearrange("v (p t) -> v t p", t=PACK)[:, planes, :]
            weigh(total[:, planes, :], source, h, d, None if prior is None else prior[:, planes, :])
            return total

        parts = []
        for h in range(HALVES):
            single = read("part%d_0" % h, h, 0, None, every)
            first = read("part%d_1" % h, h, 1, pos_sum[h], every)
            kept = every if h == 0 else alone
            second = read("part%d_2" % h, h, 2, None, kept)
            third = read("part%d_3" % h, h, 3, single, every)
            parts.append([(first, kept), (second, kept), (third, every)])
        parts[1].append((read("part1_4", 1, 2, first, joined), joined))
        q_codes = sb("q_codes", [P, R], U32, tag="part1_1")
        q_scale = sb("q_scale", [P, R], U8)
        nc.vector.quantize_mx(out=q_codes[:].bitcast(FP8X4), scales=q_scale[:], in_=q_grouped[:])
        k_codes, k_scale = [], []
        for h in range(HALVES):
            keys = bank(h, shape)
            turns = [(part, t) for part, planes in parts[h] for t in range(planes.start, planes.stop)]
            for n, (part, t) in enumerate(turns):
                nc.tensor.matmul(
                    out=keys[:, t, :], lhsT=part[:, t, :], rhs=ident[:], is_transpose=True,
                    start=(n == 0), stop=(n == len(turns) - 1),
                )
            grouped = sb("k_grouped%d" % h, [P, P * PACK], BF16)
            nc.scalar.copy(
                out=grouped[:].rearrange("p (v t) -> p v t", t=PACK),
                in_=keys[:].rearrange("p t v -> p v t"),
            )
            codes = sb("k_codes%d" % h, [P, P], U32)
            scale = sb("k_scale%d" % h, [P, P], U8)
            nc.vector.quantize_mx(out=codes[:].bitcast(FP8X4), scales=scale[:], in_=grouped[:])
            k_codes.append(codes)
            k_scale.append(scale)

        def score(target, n, h):
            nc.tensor.matmul_mx(
                out=target,
                lhsT=q_codes[:, n * P : (n + 1) * P].bitcast(FP8X4),
                lhsT_scale=q_scale[:, n * P : (n + 1) * P],
                rhs=k_codes[h][:].bitcast(FP8X4),
                rhs_scale=k_scale[h][:],
                start=True,
                stop=True,
            )

        def negate(negated, least, source, h, prior):
            nc.vector.tensor_scalar(
                out=negated[:, h * P : (h + 1) * P], in0=source, scalar1=-1.0, scalar2=prior,
                op0=ALU.mult, op1=ALU.min, accum_out=least[:],
            )

        early = bank(2, [P, EARLY_TILES, P])
        scores = [bank(3 + n, [P, P] if n < EARLY_TILES else [P, V]) for n in range(QTILES)]
        for n in range(QTILES):
            score(early[:, n, :] if n < EARLY_TILES else scores[n][:, 0:P], n, 0)
        for n in range(QTILES):
            score(scores[n][:] if n < EARLY_TILES else scores[n][:, P:V], n, 1)
        negated, first_least = [], []
        for n in range(EARLY_TILES):
            negated.append(sb("negated%d" % n, [P, V], F32, tag="k_grouped1" if n == 0 else None))
            first_least.append(sb("first_least%d" % n, [P, 1], F32))
            negate(negated[n], first_least[n], early[:, n, :], 0, None)
        for n in range(QTILES):
            shift = sb("shift%d" % n, [P, 1], F32)
            ex = sb("ex%d" % n, [P, V], F32)
            total = sb("total%d" % n, [P, 1], F32)
            if n < EARLY_TILES:
                negate(negated[n], shift, scores[n][:], 1, first_least[n][:])
                nc.scalar.activation(
                    out=ex[:], in_=negated[n][:], func=ACT.Exp, scale=-1.0, bias=shift[:], accum_out=total[:]
                )
            else:
                nc.vector.tensor_reduce(out=shift[:], in_=scores[n][:], axis=AX.X, op=ALU.max, negate=True)
                nc.scalar.activation(
                    out=ex[:], in_=scores[n][:], func=ACT.Exp, bias=shift[:], accum_out=total[:]
                )
            inverse = sb("inverse%d" % n, [P, 1], F32)
            nc.vector.reciprocal(out=inverse[:], in_=total[:])
            weights = sb("weights%d" % n, [P, V], F32)
            nc.vector.tensor_scalar(
                out=weights[:], in0=ex[:], scalar1=inverse[:], scalar2=None, op0=ALU.mult
            )
            nc.sync.dma_start(out=out[n * P : (n + 1) * P, :], in_=weights[:])
